import numpy as np, ml_dtypes
CORES = [23,119,17,113]
N = 4
BF = ml_dtypes.bfloat16
def gentries(a):
    return np.ascontiguousarray(a.reshape(8, 16, -1).transpose(0, 2, 1)).reshape(8, -1)
def gtable(e):
    e = np.asarray(e); return np.ascontiguousarray(e.reshape(8, -1, 16).transpose(0, 2, 1)).reshape(128, -1).astype(np.int32)
DR, NZ, Z, R = 2, 2, 2560, 2
ND, DD, C = N * DR, N * DR - 2, 2 * Z // R
def disks(x):
    return np.ascontiguousarray(x.astype(np.float32).astype(np.int32).reshape(N, 128, DR, NZ, Z).transpose(0, 2, 3, 1, 4)).reshape(ND, NZ, 128, Z)
def turns(pi):
    return np.ascontiguousarray(np.stack([gentries(a) for a in pi]).reshape(N, 8, DR, NZ, Z).transpose(0, 2, 3, 1, 4)).reshape(ND, NZ, 8, Z)
def follow(pa, pb):
    inv = np.zeros(Z, np.int64); inv[pb] = np.arange(Z)
    return inv, pa[inv]
def solve(w, p, a, b, ze):
    ps = w[DD].copy(); qs = w[DD + 1].copy()
    for i in range(DD):
        if i != a and i != b: ps -= w[i]; qs -= w[i][:, p[i]]
    ps = np.ascontiguousarray(ps.T) & 255; qs = np.ascontiguousarray(qs.T) & 255
    inv, nx = follow(p[a], p[b]); d = ps - qs[inv]; live = (ze == 0)[:, None]; xa = np.zeros((Z, 16), np.int32)
    for s in range(128): xa = np.where(live, d + xa[nx], 0) & 255
    return xa, (ps - xa) & 255, qs
def some_bytes(rng, *shape):
    return rng.integers(0, 256, shape, dtype=np.uint8).astype(np.int32)
def some_turns(rng):
    return rng.permuted(np.tile(np.arange(Z), (DD, NZ, 8, 1)), axis=-1)
def some_pairs(rng):
    o = rng.permutation(DD); return np.array([[o[g % DD], o[(g + rng.integers(1, DD)) % DD]] for g in range(8)])
def marks(rng, nx, gaps, first):
    m = np.zeros(Z, bool); n = nx.tolist(); seen = [False] * Z; u = 0
    for s in first + rng.permutation(Z).tolist():
        left = 0
        while not seen[s]:
            seen[s] = True
            if left == 0: m[s] = True; left = gaps[u]; u += 1
            left -= 1; s = n[s]
    return m
def write(rng, v, p, lo, far=False, first=None):
    ze = np.zeros((NZ, 8, Z), bool); qs = np.zeros((NZ, 128, Z), np.int32)
    for z in range(NZ):
        for g in range(8):
            a, b = lo[g]; k = slice(16 * g, 16 * g + 16)
            gaps = np.where(rng.random(Z) < (1 if far else 0.25), 128, rng.integers(1, 129, Z)).tolist()
            ze[z, g] = marks(rng, follow(p[a, z, g], p[b, z, g])[1], gaps, [] if first is None else first[g])
            v[a, z, k] *= ~ze[z, g]
            for i in range(DD): qs[z, k] += v[i, z, k][:, p[i, z, g]]
    ps = np.add.reduce(v, axis=0)
    for g in range(8):
        for i in lo[g]: v[i, :, 16 * g:16 * g + 16] = some_bytes(rng, NZ, 16, Z)
    w = np.concatenate([v, ps[None] & 255, qs[None] & 255]); t = np.concatenate([p, np.tile(np.arange(Z), (2, NZ, 8, 1))])
    t = t.reshape(N, DR, NZ, 8, Z).transpose(0, 3, 1, 2, 4).reshape(N, 8, -1)
    return {"x": np.ascontiguousarray(w.reshape(N, DR, NZ, 128, Z).transpose(0, 3, 1, 2, 4)).reshape(N, 128, -1).astype(np.float32).astype(BF),
            "pi": np.stack([gtable(e) for e in t]), "lost": np.stack([np.repeat(lo, 16, axis=0).astype(np.int32)] * N), "zero": np.stack([gtable(ze[q // R]) for q in range(N)])}
def setup_inputs(rng):
    return write(rng, some_bytes(rng, DD, NZ, 128, Z), some_turns(rng), some_pairs(rng))
def setup_inputs_long(rng):
    p = some_turns(rng); lo = some_pairs(rng)
    for z in range(NZ):
        for g in range(8):
            o = np.arange(Z) if g == 0 else np.arange(Z)[::-1] if g == 1 else rng.permutation(Z)
            c = np.zeros(Z, np.int64); c[o] = np.roll(o, -1); a, b = lo[g]; p[a, z, g] = c[p[b, z, g]]
    return write(rng, some_bytes(rng, DD, NZ, 128, Z), p, lo, True, [[0], [Z - 1]] + [[]] * 6)
def setup_inputs_short(rng):
    p = some_turns(rng); lo = some_pairs(rng); h = rng.permutation(8)
    for z in range(NZ):
        for u in range(6):
            g = h[u]; a, b = lo[g]; o = rng.permutation(Z); c = np.arange(Z)
            if u == 1: c[o[0::2]] = o[1::2]; c[o[1::2]] = o[0::2]
            if u == 2:
                i = 0
                while i < Z:
                    n = int(rng.integers(1, 6)); k = o[i:i + n]; c[k] = np.roll(k, -1); i += n
            if u < 3: p[a, z, g] = c[p[b, z, g]]
            if u == 3:
                for i in range(DD):
                    if i != a and i != b: p[i, z, g] = np.arange(Z)
            if u == 4: p[b, z, g] = np.arange(Z)
            if u == 5: p[a, z, g] = np.arange(Z)
    return write(rng, some_bytes(rng, DD, NZ, 128, Z), p, lo, True)
def setup_inputs_pair(rng):
    lo = np.array([[0, DD - 1] if e else [DD - 1, 0] for e in rng.permutation(8) < 4])
    return write(rng, some_bytes(rng, DD, NZ, 128, Z), some_turns(rng), lo)
def setup_inputs_spread(rng):
    v = some_bytes(rng, DD, NZ, 128, Z) & rng.choice(np.array([0, 1, 3, 15, 63, 128, 255], np.int32), (DD, NZ, 1, Z))
    v[rng.random(v.shape, dtype=np.float32) < 0.2] = 255
    return write(rng, v, some_turns(rng), some_pairs(rng))
def check_inputs(d):
    bad = []; x = d["x"].astype(np.float32); p = turns(d["pi"]); lo = d["lost"]; ze = d["zero"]
    if not ((x >= 0) & (x <= 255) & (x == np.floor(x))).all(): bad.append("bytes")
    if not (np.sort(p, axis=-1) == np.arange(Z)).all(): bad.append("permutations")
    if not (p[DD:] == np.arange(Z)).all(): bad.append("identity")
    if not ((lo >= 0) & (lo < DD)).all() or not (lo[:, :, 0] != lo[:, :, 1]).all() or not (lo == np.repeat(lo[0, ::16], 16, axis=0)).all(): bad.append("lost")
    if not ((ze == 0) | (ze == 1)).all() or not all((ze[q] == ze[q - q % R]).all() for q in range(N)): bad.append("zero")
    if bad: return bad
    v = disks(d["x"])
    for z in range(NZ):
        e = gentries(ze[z * R])
        for g in range(8):
            a, b = int(lo[0, 16 * g, 0]), int(lo[0, 16 * g, 1]); nx = follow(p[a, z, g], p[b, z, g])[1]; m = e[g][nx] == 1; first = m
            for s in range(127): m = first | m[nx]
            if not m.all(): bad.append("chains")
            xa, xb, qs = solve(v[:, z, 16 * g:16 * g + 16], p[:, z, g], a, b, e[g])
            if not (((xa[p[a, z, g]] + xb[p[b, z, g]]) & 255) == qs).all(): bad.append("sums")
    return sorted(set(bad))
def reference(x, pi, lost, zero):
    v = disks(x); p = turns(pi); y = np.zeros((N, 128, C), np.float32)
    for z in range(NZ):
        e = gentries(zero[z * R])
        for g in range(8):
            xa, xb, qs = solve(v[:, z, 16 * g:16 * g + 16], p[:, z, g], int(lost[0, 16 * g, 0]), int(lost[0, 16 * g, 1]), e[g])
            both = np.concatenate([xa, xb]).T
            for s in range(R): y[z * R + s, 16 * g:16 * g + 16] = both[:, s * C:(s + 1) * C]
    return {"y": y.astype(BF)}

@@ -1,0 +1,687 @@
+from concourse.bass import DstId, RemoteDMATransfer
+from concourse.mybir import dt, AluOpType, AxisListType, ActivationFunctionType
+
+Z = 2560
+H = Z // 2
+W = Z // 16
+NPRE = 2
+NHELP = 2
+ZS = Z + 16
+BIG = 3221225472.0
+
+SCRATCH = {
+    "xs": ("sbuf", [128, 3 * Z], "bfloat16"),
+    "xt": ("sbuf", [128, 4 * Z], "bfloat16"),
+    "gq": ("sbuf", [128, 3 * Z], "bfloat16"),
+    "pis": ("sbuf", [128, 4 * W], "int32"),
+    "pio": ("sbuf", [128, 4 * W], "float16"),
+    "pih": ("sbuf", [128, 3 * W], "float16"),
+    "losti": ("sbuf", [128, 8], "int32"),
+    "zeroi": ("sbuf", [128, W], "int32"),
+    "zb": ("sbuf", [128, W], "bfloat16"),
+    "ci": ("sbuf", [128, 8], "int32"),
+    "cf": ("sbuf", [128, 32], "float32"),
+    "mk": ("sbuf", [128, 48], "float32"),
+    "row": ("sbuf", [128, 144], "float32"),
+    "eb": ("sbuf", [128, 256], "bfloat16"),
+    "sa": ("sbuf", [128, 3 * 256], "float16"),
+    "sb": ("sbuf", [128, 3 * 128], "float16"),
+    "wq": ("sbuf", [128, 4 * 128], "bfloat16"),
+    "wp": ("sbuf", [128, 4 * 256], "bfloat16"),
+    "bx": ("sbuf", [128, 144], "bfloat16"),
+    "by": ("sbuf", [128, 144], "bfloat16"),
+    "iw": ("sbuf", [128, Z], "bfloat16"),
+    "inv": ("sbuf", [128, Z], "bfloat16"),
+    "tab": ("sbuf", [128, 3 * ZS], "bfloat16"),
+    "lst": ("sbuf", [128, 13 * W], "uint16"),
+    "qn": ("sbuf", [128, ZS], "float32"),
+    "va": ("sbuf", [128, ZS], "float32"),
+    "vb": ("sbuf", [128, ZS], "float32"),
+    "vd": ("sbuf", [128, Z], "float32"),
+    "pn": ("sbuf", [128, H], "float32"),
+    "xf": ("sbuf", [128, H], "float32"),
+    "xu": ("sbuf", [128, H], "float32"),
+    "rb": ("sbuf", [128, H], "bfloat16"),
+    "xj": ("sbuf", [128, H], "int32"),
+    "xm": ("sbuf", [128, H], "int32"),
+    "osend": ("sbuf", [128, H], "bfloat16"),
+    "okeep": ("sbuf", [128, H], "bfloat16"),
+    "oland": ("sbuf", [128, H], "bfloat16"),
+    "ps": ("psum", [128, 4096], "float32"),
+}
+SEMAPHORES = (["eV", "eS", "eP", "eG", "sent", "api", "lpi", "llo", "lze", "go", "hop0", "hop1"] + ["lx%d" % i for i in range(4)]
+              + ["at%d" % i for i in range(4)] + ["af0", "af1", "st0", "st1", "st2", "st3"] + ["du%d" % i for i in range(40)])
+
+LA, LB, LI, L0, LQ = 0, W, 2 * W, 3 * W, 10 * W
+EX = 3840
+PC = 2560
+TAB = {"pib": 0, "ta": ZS, "tb": 2 * ZS}
+
+
+def send_order(q, T, topo):
+    me = T.cores[q]
+    others = [d for d in range(len(T.cores)) if d != q]
+    off = [d for d in others if topo.chip(T.cores[d]) != topo.chip(me)]
+    on = [d for d in others if d not in off]
+    off.sort(key=lambda d: topo.die(T.cores[d]) != topo.die(me))
+    return off, on
+
+
+def helpers(q, T, topo):
+    me = T.cores[q]
+    off, _ = send_order(q, T, topo)
+    h = [c for c in topo.cores_of(me) if c not in T.cores and topo.die(c) == topo.die(me)
+         and all(topo.may_write(c, T.cores[d]) for d in off)]
+    return h[:NHELP]
+
+
+def tile_order(q, T, topo):
+    off, on = send_order(q, T, topo)
+    last = len(T.cores) - 1
+    if q == last:
+        return off + on + [q]
+    if on == [last]:
+        return [on[0], q] + off
+    return [off[0], q, off[1], on[0]]
+
+
+def expected(r, q, T, topo):
+    off, on = send_order(r, T, topo)
+    i = tile_order(r, T, topo).index(q)
+    if r == len(T.cores) - 1:
+        return [14, 17, 17, 15][i]
+    if q == r:
+        return 11
+    return [10, 0, 17, 19][i] + (6 if q in off else 0)
+
+
+def bits(engines):
+    m = 0
+    for e in engines:
+        m |= 1 << e
+    return m
+
+
+def pow2(lst):
+    n = 1
+    while 2 * n <= len(lst):
+        n *= 2
+    return lst[:n]
+
+
+def small_engines(q, T, topo):
+    me = T.cores[q]
+    off, on = send_order(q, T, topo)
+    used, small = [], {}
+    for i, d in enumerate(off):
+        e = topo.engines(me, T.cores[d])
+        used += e
+        n = len(e) // len(off)
+        small[d] = pow2(e[i * n:(i + 1) * n])
+    for i, d in enumerate(on):
+        e = [k for k in topo.engines(me, T.cores[d]) if k not in used]
+        n = len(e) // len(on)
+        small[d] = pow2(e[i * n:(i + 1) * n])
+    return small
+
+
+def hop_engines(q, i, T, topo):
+    e = topo.engines(T.cores[q], helpers(q, T, topo)[i])
+    n = len(e) // NHELP
+    return e[i * n:(i + 1) * n]
+
+
+def helper_program(g, core, T, topo):
+    for q in range(len(T.cores)):
+        hs = helpers(q, T, topo)
+        if core in hs:
+            i = hs.index(core)
+            w = Z // NHELP
+            n = 0
+            for k, d in enumerate(send_order(q, T, topo)[0]):
+                g.wait_ge(T.sem["hop%d" % k], len(hop_engines(q, i, T, topo)))
+                rid, pid, _ = topo.addr(T.cores[d])
+                g.remote_dma(T.xt[:, q * Z + i * w:q * Z + (i + 1) * w], T.xs[:, k * w:(k + 1) * w], T.sem["at%d" % q], T.sem.sent,
+                             pid, rid, topo.mask(core, T.cores[d]))
+                n += len(topo.engines(core, T.cores[d]))
+            g.wait_ge(T.sem.sent, n)
+
+
+def rank_program(g, core, T, topo):
+    q = T.rank_of(core)
+    if q is None:
+        helper_program(g, core, T, topo)
+        return
+    N = len(T.cores)
+    z, s = q // 2, q % 2
+    A = AluOpType
+    F = ActivationFunctionType
+    eng = {"V": g.vector, "S": g.scalar, "P": g.tensor, "G": g, "Y": g.sync}
+    cnt = {}
+    waited = {e: {} for e in eng}
+    log = {}
+
+    def R(name, c0, c1, p0=0, p1=128, step=1):
+        if name in TAB:
+            return ("tab", p0, p1, TAB[name] + c0, TAB[name] + c1, step)
+        return (name, p0, p1, c0, c1, step)
+
+    def ap(r):
+        if r[5] == 1:
+            return T[r[0]][r[1]:r[2], r[3]:r[4]]
+        return T[r[0]][r[1]:r[2], r[3]:r[4]:r[5]]
+
+    def span(r):
+        if r[0] == "ps":
+            return (0, 128, r[3] // 512 * 512, (r[4] + 511) // 512 * 512)
+        return r[1:5]
+
+    def wait(e, tok):
+        if waited[e].get(tok[0], 0) < tok[1]:
+            eng[e].wait_ge(T.sem[tok[0]], tok[1])
+            waited[e][tok[0]] = tok[1]
+
+    def before(e, reads, writes):
+        need = {}
+        for rs, wr in ((reads, False), (writes, True)):
+            for r in rs:
+                a = span(r)
+                for (b, bw, tok, be) in log.get(r[0], []):
+                    if a[0] < b[1] and b[0] < a[1] and a[2] < b[3] and b[2] < a[3]:
+                        if be == "P" and e == "P":
+                            continue
+                        if wr or bw or (r[0] == "ps" and be != e):
+                            need[tok[0]] = max(need.get(tok[0], 0), tok[1])
+        for k in need:
+            wait(e, (k, need[k]))
+
+    def after(e, reads, writes, tok):
+        for rs, wr in ((reads, False), (writes, True)):
+            for r in rs:
+                log.setdefault(r[0], []).append((span(r), wr, tok, e))
+
+    def op(e, fn, reads, writes):
+        before(e, reads, writes)
+        k = "e" + e
+        cnt[k] = cnt.get(k, 0) + 1
+        fn().then_inc(T.sem[k], 1)
+        after(e, reads, writes, (k, cnt[k]))
+
+    def dmas(e, sem, items):
+        tok = (sem, cnt.get(sem, 0) + 16 * len(items))
+        cnt[sem] = tok[1]
+        for (o, i, rs, ws) in items:
+            before(e, rs, ws)
+            eng[e].dma_start(o, i).then_inc(T.sem[sem], 16)
+        for (o, i, rs, ws) in items:
+            after("D", rs, ws, tok)
+
+    def landing(sem, n, regions):
+        cnt[sem] = n
+        after("D", [], regions, (sem, n))
+
+    def sc(x):
+        return ap(x) if isinstance(x, tuple) else x
+
+    def regs(*xs):
+        return [x for x in xs if isinstance(x, tuple)]
+
+    def ts(out, in0, s1, op0, s2=None, op1=None):
+        if op1 is None:
+            op("V", lambda: g.vector.tensor_scalar(ap(out), ap(in0), sc(s1), None, op0), regs(in0, s1), [out])
+        else:
+            op("V", lambda: g.vector.tensor_scalar(ap(out), ap(in0), sc(s1), sc(s2), op0, op1), regs(in0, s1, s2), [out])
+
+    def tt(out, in0, in1, o):
+        op("V", lambda: g.vector.tensor_tensor(ap(out), ap(in0), ap(in1), o), [in0, in1], [out])
+
+    def cp(e, out, in_):
+        if e == "V":
+            op("V", lambda: g.vector.tensor_copy(ap(out), ap(in_)), [in_], [out])
+        else:
+            op("S", lambda: g.scalar.activation(ap(out), ap(in_), F.Copy), [in_], [out])
+
+    def act(out, in_, func, bias=0.0, scale=1.0):
+        op("S", lambda: g.scalar.activation(ap(out), ap(in_), func, bias=sc(bias), scale=sc(scale)), regs(in_, bias, scale), [out])
+
+    def fill(out, v):
+        op("V", lambda: g.vector.memset(ap(out), v), [], [out])
+
+    def gather(e, out, win, lc, in1=None):
+        off = R("lst", lc, lc + (out[4] - out[3]) // 16)
+        if in1 is not None:
+            op("V", lambda: g.vector.tensor_tensor(ap(out), ap(win).indirect(ap(off)), ap(in1), A.add), [win, off, in1], [out])
+        elif e == "V":
+            op("V", lambda: g.vector.tensor_copy(ap(out), ap(win).indirect(ap(off))), [win, off], [out])
+        else:
+            op("S", lambda: g.scalar.activation(ap(out), ap(win).indirect(ap(off)), F.Copy), [win, off], [out])
+
+    def mms(items):
+        reads = [i[1] for i in items] + [i[2] for i in items]
+        writes = [i[0] for i in items]
+
+        def fn():
+            ins = None
+            for (o, l, r, a, b) in items:
+                ins = g.tensor.matmul(ap(o), ap(l), ap(r), a, b)
+            return ins
+        op("P", fn, reads, writes)
+
+    def col(i):
+        return R("cf", i, i + 1)
+
+    off, on = send_order(q, T, topo)
+    order = off + on
+    small_e = small_engines(q, T, topo)
+    slot = {d: i for i, d in enumerate(order)}
+    data = N - 1
+
+    landing("api", sum(len(small_engines(r, T, topo)[q]) for r in range(data) if r != q),
+            [R("pih", r * W, (r + 1) * W) for r in range(data) if r != q])
+    for r in range(N):
+        if r != q:
+            via = [T.cores[r]] if r in on else helpers(r, T, topo)
+            landing("at%d" % r, sum(len(topo.engines(c, core)) for c in via), [R("xt", r * Z, (r + 1) * Z)])
+    mate = q ^ 1
+    fin_e = topo.engines(core, T.cores[mate])
+    for i in range(2):
+        landing("af%d" % i, len(topo.engines(T.cores[mate], core)), [R("oland", i * H // 2, (i + 1) * H // 2)])
+
+    def pi_of(r, c0, c1):
+        if r == q:
+            b = 2 * s + z
+            return R("pio", b * W + c0, b * W + c1)
+        return R("pih", r * W + c0, r * W + c1)
+
+    if q < data:
+        its = [(T.pis[64 * t:64 * t + 64, 2 * W * u:2 * W * (u + 1)], T.pi[64 * u:64 * u + 64, 2 * W * t:2 * W * (t + 1)],
+                [], [R("pis", 2 * W * u, 2 * W * (u + 1), 64 * t, 64 * t + 64)]) for t in range(2) for u in range(2)]
+        dmas("Y", "lpi", its[:2])
+        dmas("S", "lpi", its[2:])
+        after("D", [], [R("pis", 0, 4 * W)], ("lpi", cnt["lpi"]))
+    dmas("S", "llo", [(T.losti[64 * t:64 * t + 64, 0:2], T.lost[64 * s:64 * s + 64, :], [], [R("losti", 0, 2, 64 * t, 64 * t + 64)]) for t in range(2)])
+    dmas("S", "lze", [(T.zeroi[0:64, :], T.zero[64 * s:64 * s + 64, :], [], [R("zeroi", 0, W, 0, 64)])])
+    seq = tile_order(q, T, topo)
+    sent = [0]
+
+    def load(d):
+        buf, c = ("xt", q * Z) if d == q else ("xs", slot[d] * Z)
+        dz, ds = d // 2, d % 2
+        dmas("Y", "lx%d" % d, [(T[buf][64 * t:64 * t + 64, c:c + Z], T.x[64 * ds:64 * ds + 64, (2 * t + dz) * Z:(2 * t + dz + 1) * Z],
+                                [], [R(buf, c, c + Z, 64 * t, 64 * t + 64)]) for t in range(2)])
+
+    def send(d):
+        c = slot[d] * Z
+        before("G", [R("xs", c, c + Z)], [])
+        if d in on:
+            rid, pid, _ = topo.addr(T.cores[d])
+            g.remote_dma(T.xt[:, q * Z:(q + 1) * Z], T.xs[:, c:c + Z], T.sem["at%d" % q], T.sem.sent, pid, rid, topo.mask(core, T.cores[d]))
+            sent[0] += len(topo.engines(core, T.cores[d]))
+            return
+        trs, w, k = [], Z // NHELP, off.index(d)
+        for i, hc in enumerate(helpers(q, T, topo)):
+            rid, pid, _ = topo.addr(hc)
+            e = hop_engines(q, i, T, topo)
+            trs.append(RemoteDMATransfer(dst_ids=[DstId(rid=rid, pnc=pid)], dma_engine_mask=bits(e), remote_sem=T.sem["hop%d" % k],
+                                         src=T.xs[:, c + i * w:c + (i + 1) * w], dst=T.xs[:, k * w:(k + 1) * w]))
+            sent[0] += len(e)
+        g.remote_dma_fused(trs, local_sem=T.sem.sent)
+
+    load(seq[0])
+    if q == data:
+        load(seq[1])
+    op("G", lambda: g.iota(T.ci[:, 0:1], [[0, 1]], 0, 1), [], [R("ci", 0, 1)])
+    op("G", lambda: g.iota(T.row[:], [[1, 144]], -16, 0, allow_small_or_imprecise_dtypes=True), [], [R("row", 0, 144)])
+
+    fill(R("inv", 0, H), 0.0)
+    p = R("ci", 0, 1)
+    ts(R("ci", 4, 5), p, 15, A.bitwise_and)
+    ts(R("ci", 5, 6), p, 6, A.arith_shift_right)
+    ts(R("ci", 1, 2), p, 63, A.bitwise_and)
+    ts(R("ci", 2, 3), p, 48, A.bitwise_and)
+    ts(R("ci", 3, 4), p, 112, A.bitwise_and)
+    fill(R("eb", 0, 256), 0.0)
+    cp("V", R("cf", 1, 6), R("ci", 1, 6))
+    ts(col(6), col(4), 0.0, A.is_equal)
+    ts(col(7), col(4), 0.0, A.not_equal)
+    ts(R("cf", 15, 18), R("row", 16, 22, step=2), col(5), A.add)
+    ts(col(9), col(6), col(5), A.mult, 20.0, A.mult)
+    ts(R("mk", 0, 41), R("row", 16, 57), col(6), A.mult)
+    if q < data:
+        ts(R("pio", 0, 4 * W), R("pis", 0, 4 * W), -1280.0, A.add)
+        before("G", [R("pio", 0, 4 * W)], [])
+        trs = []
+        for d in order:
+            rid, pid, _ = topo.addr(T.cores[d])
+            b = 2 * (d % 2) + d // 2
+            trs.append(RemoteDMATransfer(dst_ids=[DstId(rid=rid, pnc=pid)], dma_engine_mask=bits(small_e[d]), remote_sem=T.sem.api,
+                                         src=T.pio[:, b * W:(b + 1) * W], dst=T.pih[:, q * W:(q + 1) * W]))
+            sent[0] += len(small_e[d])
+        g.remote_dma_fused(trs, local_sem=T.sem.sent)
+    send(seq[0])
+    if q == data:
+        send(seq[1])
+    g.sem_inc(T.sem.go, 1)
+    g.sync.wait_ge(T.sem.go, 1)
+    for d in seq[(2 if q == data else 1):]:
+        load(d)
+    for d in seq[2:]:
+        if d != q:
+            send(d)
+
+    act(col(8), col(4), F.Relu, bias=64.0, scale=-63.0)
+    act(R("iw", 0, 64), R("row", 16, 80), F.Identity, bias=col(9), scale=col(7))
+    act(col(11), col(5), F.Identity, scale=-1.0)
+    act(col(12), col(5), F.Identity, bias=1.0, scale=-1.0)
+    for k in range(1, 4):
+        act(R("iw", 64 * k, 64 * k + 64), R("iw", 0, 64), F.Identity, bias=R("mk", k, k + 1))
+    for k in range(1, 5):
+        act(R("iw", 256 * k, 256 * k + 256), R("iw", 0, 256), F.Identity, bias=R("mk", 4 * k, 4 * k + 1))
+    cp("V", R("cf", 13, 15), R("losti", 0, 2))
+    ts(R("eb", 64, 128), R("row", 16, 80), col(1), A.is_equal)
+    ts(R("eb", 128, 192), R("row", 16, 80), col(1), A.is_equal)
+    ts(col(10), col(9), -2.0, A.mult, R("mk", 20, 21), A.add)
+    ts(R("cf", 18, 21), R("cf", 15, 18), col(13), A.is_equal)
+    ts(R("cf", 21, 24), R("cf", 15, 18), col(14), A.is_equal)
+    fill(R("inv", H, Z), 0.0)
+    tt(R("cf", 27, 30), R("cf", 18, 21), R("cf", 21, 24), A.add)
+    for r in range(data):
+        ts(R("sa", 256 * r, 256 * r + 256), R("eb", 0, 256), col(18 + r), A.mult)
+    for r in range(data):
+        ts(R("sb", 128 * r, 128 * r + 128), R("eb", 64, 192), col(21 + r), A.mult)
+    act(R("iw", H, Z), R("iw", 0, H), F.Identity, bias=col(10))
+    act(R("cf", 24, 27), R("cf", 27, 30), F.Identity, bias=1.0, scale=-1.0)
+    act(R("cf", 27, 30), R("cf", 27, 30), F.Identity, bias=-1.0)
+    for r in [q] + order:
+        act(R("wp", 256 * r, 256 * r + 256), R("eb", 0, 256), F.Identity, scale=col(27 + r if r < data else 12))
+        act(R("wq", 128 * r, 128 * r + 128), R("eb", 64, 192), F.Identity, scale=col(24 + r if r < data else 11))
+
+    def q_list(r):
+        ts(R("lst", LQ + r * W, LQ + (r + 1) * W), pi_of(r, 0, W), 1280.0, A.add)
+    if q < data:
+        q_list(q)
+    ts(R("by", 0, 80), R("row", 0, 80), col(2), A.is_equal, col(8), A.mult)
+    ts(R("by", 80, 144), R("row", 16, 80), col(2), A.is_equal, col(8), A.mult)
+
+    arrive = sorted(range(N), key=lambda r: expected(r, q, T, topo))
+    gl = [r for r in arrive if r < data]
+
+    mms([(R("ps", EX, EX + 80), R("sa", 256 * r + 128 * (1 - h), 256 * r + 128 * (2 - h)), pi_of(r, 80 * h, 80 * h + 80),
+          r == 0 and h == 0, r == data - 1 and h == 1) for r in range(data) for h in range(2)])
+    mms([(R("ps", 0, W), R("sb", 128 * r, 128 * r + 128), pi_of(r, 0, W), r == 0, r == data - 1) for r in range(data)])
+    if gl[0] != q:
+        q_list(gl[0])
+    ts(R("lst", LA, LA + 80), R("ps", EX, EX + 80), 1280.0, A.add)
+    ts(R("lst", LB, LB + W), R("ps", 0, W), 1280.0, A.add)
+    op("V", lambda: g.vector.tensor_copy(T.inv[:, 0:Z].indirect(T.lst[:, LA:LA + 80]), T.iw[:, 0:H]),
+       [R("iw", 0, H), R("lst", LA, LA + 80)], [R("inv", 0, Z)])
+    gather("S", R("pib", 0, Z), R("iw", 0, Z), LB)
+
+    grp = {}
+
+    def flags(key, total):
+        grp[key] = grp.get(key, 0) + 1
+        return grp[key] == 1, grp[key] == total
+
+    def q_mm(r, banks=range(5)):
+        src = "gq" if r < data else "xt"
+        mms([(R("ps", 512 * b, 512 * b + 512), R("wq", 128 * r, 128 * r + 128), R(src, r * Z + 512 * b, r * Z + 512 * b + 512))
+             + flags(("q", b), N) for b in banks])
+
+    def p_items(r, c0, c1, at, total):
+        return [(R("ps", at, at + c1 - c0), R("wp", 256 * r + 128 * (1 - h), 256 * r + 128 * (2 - h)),
+                 R("xt", r * Z + H * h + c0, r * Z + H * h + c1)) + flags(("p", at), total) for h in range(2)]
+
+    pieces = []
+    for r in arrive:
+        st = expected(r, q, T, topo)
+        for c in (0, 512):
+            pieces.append((st, lambda r=r, c=c: mms(p_items(r, c, c + 512, PC + c, 2 * N))))
+        if r == data:
+            for bs in ((0, 1), (3, 4), (2,)):
+                pieces.append((st, lambda r=r, bs=bs: q_mm(r, bs)))
+
+    def filler(stage, most):
+        k = 0
+        while pieces and pieces[0][0] <= stage and k < most:
+            pieces.pop(0)[1]()
+            k += 1
+
+    def extract(tab, lc, half):
+        mms([(R("ps", EX, EX + 80), R("bx", 16 - r, 144 - r), R(tab, H * half + r, H * half + H, step=16), r == 0, r == 15) for r in range(16)])
+
+    def evac(lc, half):
+        cp("V", R("lst", lc + 80 * half, lc + 80 * half + 80), R("ps", EX, EX + 80))
+
+    pend = []
+
+    def flush():
+        while pend:
+            evac(*pend.pop(0))
+
+    def both(src, dst, lin, lout, stage, nv=576):
+        win = R(src, 0, Z + 1)
+        for half in range(2):
+            c = H * half
+            gather("S", R(dst, c + nv, c + H), win, lin + (c + nv) // 16)
+            gather("V", R(dst, c, c + nv), win, lin + c // 16)
+            flush()
+            extract(dst, lout, half)
+            pend.append((lout, half))
+            filler(stage, 1)
+
+    def tile_part(e, r, c0, c1):
+        gather(e, R("gq", r * Z + c0, r * Z + c1), R("xt", r * Z, (r + 1) * Z), LQ + r * W + c0 // 16)
+
+    filler(12, 5)
+    ts(R("zb", 0, W, 0, 64), R("zeroi", 0, W, 0, 64), 4096.0, A.mult)
+    mms([(R("ps", EX, EX + W), R("by", 16 - r, 144 - r), R("inv", r, Z, step=16), r == 0, False) for r in range(16)])
+    mms([(R("ps", EX, EX + W), R("eb", 64, 192, 0, 64), R("zb", 0, W, 0, 64), False, True)])
+    ts(R("tab", Z, 3 * ZS, step=ZS), R("row", 0, 3), 0.0, A.mult, R("mk", 40, 41), A.add)
+    ts(R("bx", 0, 144), R("row", 0, 144), col(3), A.is_equal, col(8), A.mult)
+    tile_part("S", gl[0], 480, Z)
+    tile_part("V", gl[0], 0, 480)
+    ts(R("lst", LI, LI + W, 0, 64), R("ps", EX, EX + W, 0, 64), float(Z), A.min)
+    ts(R("lst", LI, LI + 80, 64, 128), R("ps", EX + 80, EX + W, 64, 128), float(Z), A.min)
+    ts(R("lst", LI + 80, LI + W, 64, 128), R("ps", EX, EX + 80, 64, 128), float(Z), A.min)
+    tabs = ["ta", "tb"]
+    step_n = [0]
+    q_mm(gl[0])
+    both("pib", "ta", LI, L0, 15)
+
+    def step(stage):
+        k = step_n[0]
+        both(tabs[k % 2], tabs[(k + 1) % 2], L0 + W * k, L0 + W * (k + 1), stage)
+        step_n[0] += 1
+    if NPRE >= 1:
+        step(17)
+    for r in gl[1:]:
+        q_list(r)
+    tile_part("S", gl[1], 1184, Z)
+    tile_part("V", gl[1], 0, 480)
+    flush()
+    filler(19, 3)
+    tile_part("V", gl[1], 480, 1184)
+    q_mm(gl[1])
+    for k in range(1, NPRE):
+        step(19)
+    fill(R("qn", Z, Z + 1), -127.5)
+    fill(R("va", Z, Z + 1), 0.0)
+    fill(R("vb", Z, Z + 1), 0.0)
+    tile_part("S", gl[2], 1280, Z)
+    tile_part("V", gl[2], 0, 480)
+    flush()
+    filler(99, 99)
+    tile_part("V", gl[2], 480, 1280)
+    cp("S", R("pn", 0, 1024), R("ps", PC, PC + 1024))
+    for bs in ((0, 1), (3, 4), (2,)):
+        q_mm(gl[2], bs)
+    for r in arrive:
+        mms(p_items(r, 1024, H, PC + 1024, 2 * N))
+    cp("V", R("qn", 0, 1024), R("ps", 0, 1024))
+    cp("S", R("qn", 1536, Z), R("ps", 1536, Z))
+    cp("V", R("qn", 1024, 1536), R("ps", 1024, 1536))
+    cp("S", R("pn", 1024, H), R("ps", PC + 1024, PC + H))
+
+    def swap(e, buf, c0, c1, h):
+        cp(e, R(buf, H + c0, H + c1, 64 * (1 - h), 64 * (2 - h)), R(buf, c0, c1, 64 * h, 64 * h + 64))
+
+    ndup = [0]
+
+    def dup(e, buf, c0, c1):
+        if e == "G":
+            op("G", lambda: g.affine_select(T.vd[:, c0:c1], T[buf][:, c0:c1], [[0, c1 - c0]], A.is_ge, 0.0, 0, 0), [R(buf, c0, c1)], [R("vd", c0, c1)])
+        else:
+            dmas("Y", "du%d" % ndup[0], [(T.vd[:, c0:c1], T[buf][:, c0:c1], [R(buf, c0, c1)], [R("vd", c0, c1)])])
+            ndup[0] += 1
+
+    def split(win, add, dst, lc, cuts, whole):
+        for i, (c0, c1) in enumerate(cuts):
+            gather("V", R(dst, c0, c1), R(win, 0, Z + 1), lc + c0 // 16, R(add, c0, c1))
+            dup("G", dst, c0, c1)
+            if i < 3:
+                swap("S", dst, c0, c1, 0)
+                swap("S", dst, c0, c1, 1)
+                if whole:
+                    dup("Y", dst, H + c0, H + c1)
+        swap("V", dst, c0, c1, 0)
+        swap("V", dst, c0, c1, 1)
+        if whole:
+            dup("Y", dst, H + c0, H + c1)
+
+    def mixed(win, dst, lc, x):
+        w = R(win, 0, Z + 1)
+        gather("V", R(dst, 0, x), w, lc, R("vd", 0, x))
+        dup("G", dst, 0, x)
+        gather("V", R(dst, x, H), w, lc + x // 16, R("vd", x, H))
+        dup("G", dst, x, 992)
+        dup("G", dst, 992, H)
+        flush()
+        swap("S", dst, x, H, 0)
+        swap("S", dst, x, H, 1)
+        gather("V", R(dst, H, H + x), w, lc + H // 16, R("vd", H, H + x))
+
+    X = H // 2
+    split("qn", "pn", "va", LI, [(0, 256), (256, 640), (640, 1024), (1024, H)], step_n[0] < 6)
+    vs = ["va", "vb"]
+    for b in range(6):
+        cur, nxt = vs[b % 2], vs[(b + 1) % 2]
+        lc = L0 + W * b
+        n = step_n[0]
+        src, dst, lin, lout = tabs[n % 2], tabs[(n + 1) % 2], L0 + W * n, L0 + W * (n + 1)
+        if n < 5:
+            def part(c0, c1):
+                gather("V", R(nxt, c0, c1), R(cur, 0, Z + 1), lc + c0 // 16, R("vd", c0, c1))
+                if n < 4 or c0 < H + X:
+                    dup("Y", nxt, c0, c1)
+            gather("S", R(dst, 0, H), R(src, 0, Z + 1), lin)
+            part(0, 512)
+            part(512, 1024)
+            flush()
+            gather("S", R(dst, H, Z), R(src, 0, Z + 1), lin + H // 16)
+            extract(dst, lout, 0)
+            part(1024, 1536)
+            part(1536, 2048)
+            part(2048, Z)
+            evac(lout, 0)
+            extract(dst, lout, 1)
+            pend.append((lout, 1))
+            step_n[0] += 1
+        elif n == 5:
+            gather("S", R(dst, 0, H), R(src, 0, Z + 1), lin)
+            mixed(cur, nxt, lc, X)
+            extract(dst, lout, 0)
+            pend.append((lout, 0))
+            step_n[0] += 1
+        else:
+            split(cur, "vd", nxt, lc, [(0, 256), (256, X), (X, 992), (992, H)], False)
+            flush()
+    flush()
+
+    cur = vs[0]
+    rid, pid, _ = topo.addr(T.cores[mate])
+    hh = H // 2
+    pc = [0, 1024]
+    qc = [2048, 3072]
+
+    def last(i):
+        gather("V", R("xf", i * hh, (i + 1) * hh), R(cur, 0, Z + 1), L0 + 6 * W + i * hh // 16, R("vd", i * hh, (i + 1) * hh))
+
+    def p_psum(i):
+        act(R("ps", pc[i], pc[i] + hh), R("pn", i * hh, (i + 1) * hh), F.Identity, bias=-127.5)
+
+    def sub_a(i):
+        c0, c1 = i * hh, (i + 1) * hh
+        tt(R("xj", c0, c1), R("ps", pc[i], pc[i] + hh), R("xf", c0, c1), A.subtract)
+
+    def res_a(out, i):
+        c0, c1 = i * hh, (i + 1) * hh
+        ts(R("xm", c0, c1), R("xj", c0, c1), 255, A.bitwise_and)
+        cp("V", R(out, c0, c1), R("xm", c0, c1))
+
+    def round_b(i):
+        c0, c1 = i * hh, (i + 1) * hh
+        act(R("xu", c0, c1), R("xf", c0, c1), F.Identity, bias=BIG)
+        act(R("ps", qc[i], qc[i] + hh), R("xu", c0, c1), F.Identity, bias=-BIG)
+
+    def rest_b(i):
+        c0, c1 = i * hh, (i + 1) * hh
+        tt(R("rb", c0, c1), R("xf", c0, c1), R("ps", qc[i], qc[i] + hh), A.subtract)
+
+    def res_b(out, i):
+        act(R(out, i * hh, (i + 1) * hh), R("rb", i * hh, (i + 1) * hh), F.Identity, bias=127.5)
+
+    def hand(i):
+        c0, c1 = i * hh, (i + 1) * hh
+        before("G", [R("osend", c0, c1)], [])
+        g.remote_dma(T.oland[:, c0:c1], T.osend[:, c0:c1], T.sem["af%d" % i], T.sem.sent, pid, rid, bits(fin_e))
+        sent[0] += len(fin_e)
+
+    def store(e, sem, buf, rows, i):
+        c0, c1 = i * hh, (i + 1) * hh
+        dmas(e, sem, [(T.y[64 * rows:64 * rows + 64, H * h + c0:H * h + c1], T[buf][64 * h:64 * h + 64, c0:c1],
+                       [R(buf, c0, c1, 64 * h, 64 * h + 64)], []) for h in range(2)])
+
+    p_psum(0)
+    if s == 0:
+        last(0)
+        round_b(0)
+        last(1)
+        round_b(1)
+        rest_b(0)
+        ts(R("osend", 0, hh), R("rb", 0, hh), 127.5, A.add)
+        hand(0)
+        sub_a(0)
+        rest_b(1)
+        res_b("osend", 1)
+        hand(1)
+        p_psum(1)
+        res_a("okeep", 0)
+        store("S", "st0", "okeep", s, 0)
+        sub_a(1)
+        res_a("okeep", 1)
+        store("S", "st1", "okeep", s, 1)
+    else:
+        last(0)
+        round_b(0)
+        p_psum(1)
+        sub_a(0)
+        res_a("osend", 0)
+        hand(0)
+        last(1)
+        round_b(1)
+        sub_a(1)
+        res_a("osend", 1)
+        hand(1)
+        rest_b(0)
+        res_b("okeep", 0)
+        store("S", "st0", "okeep", s, 0)
+        rest_b(1)
+        ts(R("okeep", hh, H), R("rb", hh, H), 127.5, A.add)
+        store("S", "st1", "okeep", s, 1)
+    store("Y", "st2", "oland", 1 - s, 0)
+    store("Y", "st3", "oland", 1 - s, 1)
+    cnt["sent"] = sent[0]
+    for k in cnt:
+        if cnt[k]:
+            wait("G", (k, cnt[k]))

@@ -4,10 +4,19 @@ from concourse.mybir import dt, AluOpType, AxisListType, ActivationFunctionType
 Z = 2560
 H = Z // 2
 W = Z // 16
-NPRE = 2
+NPRE = 0
 NHELP = 2
+FIRST = 2
+EARLY = 1
+DIRECT = 0
+T0 = 1024
 ZS = Z + 16
-BIG = 3221225472.0
+TOP = 2147483648.0
+LIFT = 1536.0
+ROUND_PTR = (512, [(256, "D", "G"), (256, "D", "G"), (256, "S", "G")], 512)
+ROUND_END = (384, [(256, "D", "G"), (256, "D", "G"), (384, "S", "G")], 512)
+ROUND_FREE = (288, [(224, "S", "G"), (384, "S", "G"), (384, "S", "G")], 0)
+FIN = [(0, 512), (512, 1024), (1024, H)]
 
 SCRATCH = {
     "xs": ("sbuf", [128, 3 * Z], "bfloat16"),
@@ -19,26 +28,32 @@ SCRATCH = {
     "losti": ("sbuf", [128, 8], "int32"),
     "zeroi": ("sbuf", [128, W], "int32"),
     "zb": ("sbuf", [128, W], "bfloat16"),
+    "zf": ("sbuf", [128, 2 * W], "float32"),
     "ci": ("sbuf", [128, 8], "int32"),
-    "cf": ("sbuf", [128, 32], "float32"),
-    "mk": ("sbuf", [128, 48], "float32"),
-    "row": ("sbuf", [128, 144], "float32"),
+    "cf": ("sbuf", [128, 64], "float32"),
+    "mk": ("sbuf", [128, 80], "float32"),
+    "row": ("sbuf", [128, 176], "float32"),
     "eb": ("sbuf", [128, 256], "bfloat16"),
+    "en": ("sbuf", [128, 128], "bfloat16"),
+    "ex": ("sbuf", [128, 128], "bfloat16"),
+    "ef": ("sbuf", [128, 128], "float32"),
     "sa": ("sbuf", [128, 3 * 256], "float16"),
     "sb": ("sbuf", [128, 3 * 128], "float16"),
-    "wq": ("sbuf", [128, 4 * 128], "bfloat16"),
+    "wq": ("sbuf", [128, 128], "bfloat16"),
     "wp": ("sbuf", [128, 4 * 256], "bfloat16"),
     "bx": ("sbuf", [128, 144], "bfloat16"),
+    "bc": ("sbuf", [128, 144], "bfloat16"),
     "by": ("sbuf", [128, 144], "bfloat16"),
-    "iw": ("sbuf", [128, Z], "bfloat16"),
+    "iw": ("sbuf", [128, ZS], "bfloat16"),
+    "iz": ("sbuf", [128, Z], "bfloat16"),
     "inv": ("sbuf", [128, Z], "bfloat16"),
     "tab": ("sbuf", [128, 3 * ZS], "bfloat16"),
-    "lst": ("sbuf", [128, 13 * W], "uint16"),
+    "lst": ("sbuf", [128, 14 * W], "uint16"),
     "qn": ("sbuf", [128, ZS], "float32"),
     "va": ("sbuf", [128, ZS], "float32"),
     "vb": ("sbuf", [128, ZS], "float32"),
     "vd": ("sbuf", [128, Z], "float32"),
-    "pn": ("sbuf", [128, H], "float32"),
+    "pn": ("sbuf", [128, Z], "float32"),
     "xf": ("sbuf", [128, H], "float32"),
     "xu": ("sbuf", [128, H], "float32"),
     "rb": ("sbuf", [128, H], "bfloat16"),
@@ -50,11 +65,12 @@ SCRATCH = {
     "ps": ("psum", [128, 4096], "float32"),
 }
 SEMAPHORES = (["eV", "eS", "eP", "eG", "sent", "api", "lpi", "llo", "lze", "go", "hop0", "hop1"] + ["lx%d" % i for i in range(4)]
-              + ["at%d" % i for i in range(4)] + ["af0", "af1", "st0", "st1", "st2", "st3"] + ["du%d" % i for i in range(40)])
+              + ["at%d" % i for i in range(4)] + ["af%d" % i for i in range(4)] + ["st%d" % i for i in range(8)] + ["du%d" % i for i in range(70)])
 
-LA, LB, LI, L0, LQ = 0, W, 2 * W, 3 * W, 10 * W
-EX = 3840
+LA, LB, LI, L0, LQ, LZ = 0, W, 2 * W, 3 * W, 10 * W, 13 * W
+EX = 3584
 PC = 2560
+PD = 1024
 TAB = {"pib": 0, "ta": ZS, "tb": 2 * ZS}
 
 
@@ -77,22 +93,16 @@ def helpers(q, T, topo):
 
 def tile_order(q, T, topo):
     off, on = send_order(q, T, topo)
-    last = len(T.cores) - 1
-    if q == last:
-        return off + on + [q]
-    if on == [last]:
-        return [on[0], q] + off
-    return [off[0], q, off[1], on[0]]
+    if on == [len(T.cores) - 1]:
+        return [off[0], on[0], off[1], q]
+    return off + on + [q]
 
 
 def expected(r, q, T, topo):
     off, on = send_order(r, T, topo)
-    i = tile_order(r, T, topo).index(q)
-    if r == len(T.cores) - 1:
-        return [14, 17, 17, 15][i]
-    if q == r:
-        return 11
-    return [10, 0, 17, 19][i] + (6 if q in off else 0)
+    if q in off:
+        return 14 + 3 * off.index(q)
+    return 12 if (q == r) == (q == len(T.cores) - 1) else 11
 
 
 def bits(engines):
@@ -139,12 +149,15 @@ def helper_program(g, core, T, topo):
             w = Z // NHELP
             n = 0
             for k, d in enumerate(send_order(q, T, topo)[0]):
+                if k < DIRECT:
+                    continue
                 g.wait_ge(T.sem["hop%d" % k], len(hop_engines(q, i, T, topo)))
                 rid, pid, _ = topo.addr(T.cores[d])
                 g.remote_dma(T.xt[:, q * Z + i * w:q * Z + (i + 1) * w], T.xs[:, k * w:(k + 1) * w], T.sem["at%d" % q], T.sem.sent,
                              pid, rid, topo.mask(core, T.cores[d]))
                 n += len(topo.engines(core, T.cores[d]))
-            g.wait_ge(T.sem.sent, n)
+            if n:
+                g.wait_ge(T.sem.sent, n)
 
 
 def rank_program(g, core, T, topo):
@@ -166,7 +179,9 @@ def rank_program(g, core, T, topo):
             return ("tab", p0, p1, TAB[name] + c0, TAB[name] + c1, step)
         return (name, p0, p1, c0, c1, step)
 
-    def ap(r):
+    def ap(r, pstep=1):
+        if pstep > 1:
+            return T[r[0]][r[1]:r[2]:pstep, r[3]:r[4]]
         if r[5] == 1:
             return T[r[0]][r[1]:r[2], r[3]:r[4]]
         return T[r[0]][r[1]:r[2], r[3]:r[4]:r[5]]
@@ -241,8 +256,20 @@ def rank_program(g, core, T, topo):
         else:
             op("S", lambda: g.scalar.activation(ap(out), ap(in_), F.Copy), [in_], [out])
 
-    def act(out, in_, func, bias=0.0, scale=1.0):
+    def act(out, in_, func=F.Identity, bias=0.0, scale=1.0):
         op("S", lambda: g.scalar.activation(ap(out), ap(in_), func, bias=sc(bias), scale=sc(scale)), regs(in_, bias, scale), [out])
+
+    def plus(e, out, in_, v):
+        if e == "V":
+            ts(out, in_, v, A.add)
+        else:
+            act(out, in_, bias=v)
+
+    def minus(e, out, in_):
+        if e == "V":
+            ts(out, in_, -1.0, A.mult)
+        else:
+            act(out, in_, scale=-1.0)
 
     def fill(out, v):
         op("V", lambda: g.vector.memset(ap(out), v), [], [out])
@@ -267,8 +294,17 @@ def rank_program(g, core, T, topo):
             return ins
         op("P", fn, reads, writes)
 
-    def col(i):
-        return R("cf", i, i + 1)
+    def col(i, n=1):
+        return R("cf", i, i + n)
+
+    ndma = [0]
+
+    def copies(pairs, pstep=1):
+        dmas("Y", "du%d" % ndma[0], [(ap(o, pstep), ap(i, pstep), [i], [o]) for (o, i) in pairs])
+        ndma[0] += 1
+
+    def crossed(buf, c0, c1):
+        return [(R(buf, H + c0, H + c1, 64 * (1 - h), 64 * (2 - h)), R(buf, c0, c1, 64 * h, 64 * h + 64)) for h in range(2)]
 
     off, on = send_order(q, T, topo)
     order = off + on
@@ -280,12 +316,12 @@ def rank_program(g, core, T, topo):
             [R("pih", r * W, (r + 1) * W) for r in range(data) if r != q])
     for r in range(N):
         if r != q:
-            via = [T.cores[r]] if r in on else helpers(r, T, topo)
+            via = [T.cores[r]] if r in on or send_order(r, T, topo)[0].index(q) < DIRECT else helpers(r, T, topo)
             landing("at%d" % r, sum(len(topo.engines(c, core)) for c in via), [R("xt", r * Z, (r + 1) * Z)])
     mate = q ^ 1
     fin_e = topo.engines(core, T.cores[mate])
-    for i in range(2):
-        landing("af%d" % i, len(topo.engines(T.cores[mate], core)), [R("oland", i * H // 2, (i + 1) * H // 2)])
+    for i, (c0, c1) in enumerate(FIN):
+        landing("af%d" % i, len(topo.engines(T.cores[mate], core)), [R("oland", c0, c1)])
 
     def pi_of(r, c0, c1):
         if r == q:
@@ -300,7 +336,7 @@ def rank_program(g, core, T, topo):
         dmas("S", "lpi", its[2:])
         after("D", [], [R("pis", 0, 4 * W)], ("lpi", cnt["lpi"]))
     dmas("S", "llo", [(T.losti[64 * t:64 * t + 64, 0:2], T.lost[64 * s:64 * s + 64, :], [], [R("losti", 0, 2, 64 * t, 64 * t + 64)]) for t in range(2)])
-    dmas("S", "lze", [(T.zeroi[0:64, :], T.zero[64 * s:64 * s + 64, :], [], [R("zeroi", 0, W, 0, 64)])])
+    dmas("S", "lze", [(T.zeroi[64 * t:64 * t + 64, :], T.zero[64 * s:64 * s + 64, :], [], [R("zeroi", 0, W, 64 * t, 64 * t + 64)]) for t in range(1 + s)])
     seq = tile_order(q, T, topo)
     sent = [0]
 
@@ -313,7 +349,7 @@ def rank_program(g, core, T, topo):
     def send(d):
         c = slot[d] * Z
         before("G", [R("xs", c, c + Z)], [])
-        if d in on:
+        if d in on or off.index(d) < DIRECT:
             rid, pid, _ = topo.addr(T.cores[d])
             g.remote_dma(T.xt[:, q * Z:(q + 1) * Z], T.xs[:, c:c + Z], T.sem["at%d" % q], T.sem.sent, pid, rid, topo.mask(core, T.cores[d]))
             sent[0] += len(topo.engines(core, T.cores[d]))
@@ -327,12 +363,12 @@ def rank_program(g, core, T, topo):
             sent[0] += len(e)
         g.remote_dma_fused(trs, local_sem=T.sem.sent)
 
-    load(seq[0])
-    if q == data:
-        load(seq[1])
+    for d in seq[:FIRST]:
+        load(d)
     op("G", lambda: g.iota(T.ci[:, 0:1], [[0, 1]], 0, 1), [], [R("ci", 0, 1)])
-    op("G", lambda: g.iota(T.row[:], [[1, 144]], -16, 0, allow_small_or_imprecise_dtypes=True), [], [R("row", 0, 144)])
+    op("G", lambda: g.iota(T.row[:], [[1, 176]], -16, 0, allow_small_or_imprecise_dtypes=True), [], [R("row", 0, 176)])
 
+    EQ = 32
     fill(R("inv", 0, H), 0.0)
     p = R("ci", 0, 1)
     ts(R("ci", 4, 5), p, 15, A.bitwise_and)
@@ -341,12 +377,15 @@ def rank_program(g, core, T, topo):
     ts(R("ci", 2, 3), p, 48, A.bitwise_and)
     ts(R("ci", 3, 4), p, 112, A.bitwise_and)
     fill(R("eb", 0, 256), 0.0)
-    cp("V", R("cf", 1, 6), R("ci", 1, 6))
-    ts(col(6), col(4), 0.0, A.is_equal)
-    ts(col(7), col(4), 0.0, A.not_equal)
-    ts(R("cf", 15, 18), R("row", 16, 22, step=2), col(5), A.add)
-    ts(col(9), col(6), col(5), A.mult, 20.0, A.mult)
-    ts(R("mk", 0, 41), R("row", 16, 57), col(6), A.mult)
+    cp("V", col(1, 5), R("ci", 1, 6))
+    cp("V", col(54), p)
+    ts(col(EQ, 16), R("row", 16, 32), col(4), A.is_equal)
+    ts(col(15, 3), R("row", 16, 22, step=2), col(5), A.add)
+    ts(col(6), col(EQ), col(EQ + 1), A.add, col(EQ + 4), A.add)
+    ts(col(8), col(EQ + 1), col(5), A.mult, col(EQ + 4), A.add)
+    ts(col(7), col(EQ), col(EQ + 4), A.subtract)
+    ts(R("mk", 0, 65), R("row", 16, 81), col(6), A.mult)
+    ts(col(9), col(8), 20.0, A.mult)
     if q < data:
         ts(R("pio", 0, 4 * W), R("pis", 0, 4 * W), -1280.0, A.add)
         before("G", [R("pio", 0, 4 * W)], [])
@@ -358,50 +397,69 @@ def rank_program(g, core, T, topo):
                                          src=T.pio[:, b * W:(b + 1) * W], dst=T.pih[:, q * W:(q + 1) * W]))
             sent[0] += len(small_e[d])
         g.remote_dma_fused(trs, local_sem=T.sem.sent)
-    send(seq[0])
-    if q == data:
-        send(seq[1])
-    g.sem_inc(T.sem.go, 1)
-    g.sync.wait_ge(T.sem.go, 1)
-    for d in seq[(2 if q == data else 1):]:
+    for d in seq[:EARLY]:
+        send(d)
+    if FIRST < N:
+        g.sem_inc(T.sem.go, 1)
+        g.sync.wait_ge(T.sem.go, 1)
+    for d in seq[FIRST:]:
         load(d)
-    for d in seq[2:]:
+    for d in seq[EARLY:]:
         if d != q:
             send(d)
 
-    act(col(8), col(4), F.Relu, bias=64.0, scale=-63.0)
-    act(R("iw", 0, 64), R("row", 16, 80), F.Identity, bias=col(9), scale=col(7))
-    act(col(11), col(5), F.Identity, scale=-1.0)
-    act(col(12), col(5), F.Identity, bias=1.0, scale=-1.0)
+    act(R("iw", 0, 64), R("row", 16, 80), bias=col(9), scale=col(EQ + 8))
+    act(col(10), col(7), scale=20.0)
+    act(col(12), col(5), bias=1.0, scale=-1.0)
     for k in range(1, 4):
-        act(R("iw", 64 * k, 64 * k + 64), R("iw", 0, 64), F.Identity, bias=R("mk", k, k + 1))
+        act(R("iw", 64 * k, 64 * k + 64), R("iw", 0, 64), bias=R("mk", k, k + 1))
     for k in range(1, 5):
-        act(R("iw", 256 * k, 256 * k + 256), R("iw", 0, 256), F.Identity, bias=R("mk", 4 * k, 4 * k + 1))
-    cp("V", R("cf", 13, 15), R("losti", 0, 2))
+        act(R("iw", 256 * k, 256 * k + 256), R("iw", 0, 256), bias=R("mk", 4 * k, 4 * k + 1))
+    cp("V", col(13, 2), R("losti", 0, 2))
     ts(R("eb", 64, 128), R("row", 16, 80), col(1), A.is_equal)
     ts(R("eb", 128, 192), R("row", 16, 80), col(1), A.is_equal)
-    ts(col(10), col(9), -2.0, A.mult, R("mk", 20, 21), A.add)
-    ts(R("cf", 18, 21), R("cf", 15, 18), col(13), A.is_equal)
-    ts(R("cf", 21, 24), R("cf", 15, 18), col(14), A.is_equal)
-    fill(R("inv", H, Z), 0.0)
-    tt(R("cf", 27, 30), R("cf", 18, 21), R("cf", 21, 24), A.add)
+    ts(col(18, 3), col(15, 3), col(13 + s), A.is_equal)
+    ts(col(21, 3), col(15, 3), col(14 - s), A.is_equal)
+    if s == 1:
+        cp("V", R("iw", Z, Z + 1), R("mk", 64, 65))
+        ts(R("zf", 0, W), R("row", 16, 16 + W), 16.0, A.mult, col(4), A.add)
+    tt(col(24, 3), col(18, 3), col(21, 3), A.add)
+    if s == 1:
+        ts(R("zf", W, 2 * W), R("zeroi", 0, W), float(Z), A.mult)
+    ts(col(27, 3), col(24, 3), -1.0, A.add)
+    if s == 1:
+        tt(R("zf", 0, W), R("zf", 0, W), R("zf", W, 2 * W), A.max)
+    ts(R("iw", H, Z), R("iw", 0, H), col(10), A.add)
+    for r in range(N):
+        act(R("wp", 256 * r, 256 * r + 256), R("eb", 0, 256), scale=col(27 + r if r < data else 12))
+    if s == 1:
+        cp("V", R("lst", LZ, LZ + W), R("zf", 0, W))
+        gather("S", R("iz", 960, Z), R("iw", 0, Z + 1), LZ + 60)
     for r in range(data):
         ts(R("sa", 256 * r, 256 * r + 256), R("eb", 0, 256), col(18 + r), A.mult)
     for r in range(data):
         ts(R("sb", 128 * r, 128 * r + 128), R("eb", 64, 192), col(21 + r), A.mult)
-    act(R("iw", H, Z), R("iw", 0, H), F.Identity, bias=col(10))
-    act(R("cf", 24, 27), R("cf", 27, 30), F.Identity, bias=1.0, scale=-1.0)
-    act(R("cf", 27, 30), R("cf", 27, 30), F.Identity, bias=-1.0)
-    for r in [q] + order:
-        act(R("wp", 256 * r, 256 * r + 256), R("eb", 0, 256), F.Identity, scale=col(27 + r if r < data else 12))
-        act(R("wq", 128 * r, 128 * r + 128), R("eb", 64, 192), F.Identity, scale=col(24 + r if r < data else 11))
+    fill(R("inv", H, Z), 0.0)
+    if s == 1:
+        gather("V", R("iz", 0, 960), R("iw", 0, Z + 1), LZ)
+    act(R("wq", 0, 128), R("eb", 64, 192), scale=col(5))
+    act(col(48, 5), col(EQ, 5), bias=col(EQ + 8), scale=64.0)
+    act(col(56), col(7), scale=col(5))
+    act(col(53), col(5), bias=col(3), scale=-128.0)
+    act(col(55), col(5), bias=col(54), scale=-128.0)
+    act(col(30), col(56), bias=col(48), scale=-64.0)
+    act(col(31), col(56), bias=col(52), scale=64.0)
+    act(col(53), col(53), bias=64.0)
+    act(col(55), col(55), bias=64.0)
 
     def q_list(r):
         ts(R("lst", LQ + r * W, LQ + (r + 1) * W), pi_of(r, 0, W), 1280.0, A.add)
     if q < data:
         q_list(q)
-    ts(R("by", 0, 80), R("row", 0, 80), col(2), A.is_equal, col(8), A.mult)
-    ts(R("by", 80, 144), R("row", 16, 80), col(2), A.is_equal, col(8), A.mult)
+    if s == 0:
+        ts(R("zb", 0, W, 0, 64), R("zeroi", 0, W, 0, 64), 4096.0, A.mult)
+    ts(R("by", 0, 80), R("row", 0, 80), col(2), A.is_equal, col(49), A.mult)
+    ts(R("by", 80, 144), R("row", 16, 80), col(2), A.is_equal, col(49), A.mult)
 
     arrive = sorted(range(N), key=lambda r: expected(r, q, T, topo))
     gl = [r for r in arrive if r < data]
@@ -409,13 +467,13 @@ def rank_program(g, core, T, topo):
     mms([(R("ps", EX, EX + 80), R("sa", 256 * r + 128 * (1 - h), 256 * r + 128 * (2 - h)), pi_of(r, 80 * h, 80 * h + 80),
           r == 0 and h == 0, r == data - 1 and h == 1) for r in range(data) for h in range(2)])
     mms([(R("ps", 0, W), R("sb", 128 * r, 128 * r + 128), pi_of(r, 0, W), r == 0, r == data - 1) for r in range(data)])
-    if gl[0] != q:
-        q_list(gl[0])
     ts(R("lst", LA, LA + 80), R("ps", EX, EX + 80), 1280.0, A.add)
     ts(R("lst", LB, LB + W), R("ps", 0, W), 1280.0, A.add)
+    if gl[0] != q:
+        q_list(gl[0])
     op("V", lambda: g.vector.tensor_copy(T.inv[:, 0:Z].indirect(T.lst[:, LA:LA + 80]), T.iw[:, 0:H]),
        [R("iw", 0, H), R("lst", LA, LA + 80)], [R("inv", 0, Z)])
-    gather("S", R("pib", 0, Z), R("iw", 0, Z), LB)
+    gather("S", R("pib", 0, Z), R("iz" if s else "iw", 0, Z), LB)
 
     grp = {}
 
@@ -424,263 +482,249 @@ def rank_program(g, core, T, topo):
         return grp[key] == 1, grp[key] == total
 
     def q_mm(r, banks=range(5)):
-        src = "gq" if r < data else "xt"
-        mms([(R("ps", 512 * b, 512 * b + 512), R("wq", 128 * r, 128 * r + 128), R(src, r * Z + 512 * b, r * Z + 512 * b + 512))
-             + flags(("q", b), N) for b in banks])
+        src, wt = ("gq", R("wp", 256 * r + 64, 256 * r + 192)) if r < data else ("xt", R("wq", 0, 128))
+        mms([(R("ps", 512 * b, 512 * b + 512), wt, R(src, r * Z + 512 * b, r * Z + 512 * b + 512)) + flags(("q", b), N) for b in banks])
 
-    def p_items(r, c0, c1, at, total):
-        return [(R("ps", at, at + c1 - c0), R("wp", 256 * r + 128 * (1 - h), 256 * r + 128 * (2 - h)),
-                 R("xt", r * Z + H * h + c0, r * Z + H * h + c1)) + flags(("p", at), total) for h in range(2)]
+    emitted = []
 
-    pieces = []
-    for r in arrive:
-        st = expected(r, q, T, topo)
-        for c in (0, 512):
-            pieces.append((st, lambda r=r, c=c: mms(p_items(r, c, c + 512, PC + c, 2 * N))))
-        if r == data:
-            for bs in ((0, 1), (3, 4), (2,)):
-                pieces.append((st, lambda r=r, bs=bs: q_mm(r, bs)))
+    def p_mm(r, chunks):
+        for (c0, c1) in chunks:
+            if (r, c0) not in emitted:
+                emitted.append((r, c0))
+                mms([(R("ps", PC + c0, PC + c1), R("wp", 256 * r + 128 * (1 - h), 256 * r + 128 * (2 - h)),
+                      R("xt", r * Z + H * h + c0, r * Z + H * h + c1)) + flags(("p", c0), 2 * N) for h in range(2)])
 
-    def filler(stage, most):
-        k = 0
-        while pieces and pieces[0][0] <= stage and k < most:
-            pieces.pop(0)[1]()
-            k += 1
+    def sums_upto(r, chunks):
+        for x in arrive[:arrive.index(r) + 1]:
+            p_mm(x, chunks)
+            if x == data and (x, -1) not in emitted:
+                emitted.append((x, -1))
+                for bs in ((0, 3), (1, 4), (2,)):
+                    q_mm(x, bs)
 
-    def extract(tab, lc, half):
-        mms([(R("ps", EX, EX + 80), R("bx", 16 - r, 144 - r), R(tab, H * half + r, H * half + H, step=16), r == 0, r == 15) for r in range(16)])
+    plan = [ROUND_PTR if NPRE + i < 5 else ROUND_END if NPRE + i == 5 else ROUND_FREE for i in range(7)] + [(0, [], 0)]
 
-    def evac(lc, half):
-        cp("V", R("lst", lc + 80 * half, lc + 80 * half + 80), R("ps", EX, EX + 80))
+    def extract(tab, c0, c1, at, mat="bx"):
+        mms([(R("ps", at, at + (c1 - c0) // 16), R(mat, 16 - r, 144 - r), R(tab, c0 + r, c1, step=16), r == 0, r == 15) for r in range(16)])
 
-    pend = []
+    pend, late = [], []
 
     def flush():
         while pend:
-            evac(*pend.pop(0))
+            lc, n, at = pend.pop(0)
+            ts(R("lst", lc, lc + n), R("ps", at, at + n), float(Z), A.min)
 
-    def both(src, dst, lin, lout, stage, nv=576):
+    tabs = ["ta", "tb"]
+    level = [-1]
+    fresh = ["ta", "tb"]
+
+    def double(at, nv):
+        n = level[0]
+        src, lin = (tabs[n % 2], L0 + W * n) if n >= 0 else ("pib", LI)
+        dst, lout = tabs[(n + 1) % 2], L0 + W * (n + 1)
+        level[0] += 1
         win = R(src, 0, Z + 1)
-        for half in range(2):
-            c = H * half
-            gather("S", R(dst, c + nv, c + H), win, lin + (c + nv) // 16)
-            gather("V", R(dst, c, c + nv), win, lin + c // 16)
-            flush()
-            extract(dst, lout, half)
-            pend.append((lout, half))
-            filler(stage, 1)
+        gather("S", R(dst, nv, H), win, lin + nv // 16)
+        gather("V", R(dst, 0, nv), win, lin)
+        copies(crossed(dst, 0, H), 1 if dst in fresh else 4)
+        if dst in fresh:
+            fresh.remove(dst)
+        extract(dst, 0, H, at)
+        pend.append((lout, 80, at))
+        C = plan[n + 2][0]
+        extract(dst, H - C, H, at + 80, "bc")
+        pend.append((lout + (Z - C) // 16, C // 16, at + 80))
 
     def tile_part(e, r, c0, c1):
         gather(e, R("gq", r * Z + c0, r * Z + c1), R("xt", r * Z, (r + 1) * Z), LQ + r * W + c0 // 16)
 
-    filler(12, 5)
-    ts(R("zb", 0, W, 0, 64), R("zeroi", 0, W, 0, 64), 4096.0, A.mult)
-    mms([(R("ps", EX, EX + W), R("by", 16 - r, 144 - r), R("inv", r, Z, step=16), r == 0, False) for r in range(16)])
-    mms([(R("ps", EX, EX + W), R("eb", 64, 192, 0, 64), R("zb", 0, W, 0, 64), False, True)])
-    ts(R("tab", Z, 3 * ZS, step=ZS), R("row", 0, 3), 0.0, A.mult, R("mk", 40, 41), A.add)
-    ts(R("bx", 0, 144), R("row", 0, 144), col(3), A.is_equal, col(8), A.mult)
-    tile_part("S", gl[0], 480, Z)
+    p_mm(arrive[0], FIN[:2])
+    mms([(R("ps", EX, EX + W), R("by", 16 - r, 144 - r), R("inv", r, Z, step=16), r == 0, r == 15 and s == 1) for r in range(16)])
+    if s == 0:
+        mms([(R("ps", EX, EX + W), R("eb", 64, 192, 0, 64), R("zb", 0, W, 0, 64), False, True)])
+    ts(R("tab", Z, 3 * ZS, step=ZS), R("row", 0, 3), 0.0, A.mult, R("mk", 64, 65), A.add)
+    ts(R("bx", 0, 144), R("row", 0, 144), col(3), A.is_equal, col(30), A.mult)
+    ts(R("bc", 0, 144), R("row", 0, 144), col(53), A.is_equal, col(31), A.mult)
+    tile_part("S", gl[0], T0, Z)
     tile_part("V", gl[0], 0, 480)
-    ts(R("lst", LI, LI + W, 0, 64), R("ps", EX, EX + W, 0, 64), float(Z), A.min)
-    ts(R("lst", LI, LI + 80, 64, 128), R("ps", EX + 80, EX + W, 64, 128), float(Z), A.min)
-    ts(R("lst", LI + 80, LI + W, 64, 128), R("ps", EX, EX + 80, 64, 128), float(Z), A.min)
-    tabs = ["ta", "tb"]
-    step_n = [0]
-    q_mm(gl[0])
-    both("pib", "ta", LI, L0, 15)
-
-    def step(stage):
-        k = step_n[0]
-        both(tabs[k % 2], tabs[(k + 1) % 2], L0 + W * k, L0 + W * (k + 1), stage)
-        step_n[0] += 1
-    if NPRE >= 1:
-        step(17)
+    for c in (0, 80):
+        for h in range(2):
+            ts(R("lst", LI + c, LI + c + 80, 64 * h, 64 * h + 64), R("ps", EX + (c + 80 * h) % W, EX + (c + 80 * h) % W + 80, 64 * h, 64 * h + 64),
+               float(Z), A.min)
+    sums_upto(arrive[1], FIN[:2])
+    double(EX + 256, 576)
+    mid = (480 + T0) // 64 * 32
+    tile_part("S", gl[0], mid, T0)
+    tile_part("V", gl[0], 480, mid)
     for r in gl[1:]:
         q_list(r)
-    tile_part("S", gl[1], 1184, Z)
-    tile_part("V", gl[1], 0, 480)
-    flush()
-    filler(19, 3)
-    tile_part("V", gl[1], 480, 1184)
-    q_mm(gl[1])
-    for k in range(1, NPRE):
-        step(19)
-    fill(R("qn", Z, Z + 1), -127.5)
+    q_mm(gl[0])
+    ts(R("ex", 0, 128), R("row", 16, 144), col(55), A.is_equal)
+    ts(R("en", 0, 128), R("row", 16, 144), col(54), A.is_equal, -1.0, A.mult)
+    ts(R("ef", 0, 128), R("row", 16, 144), col(54), A.is_equal)
+    fill(R("qn", Z, Z + 1), 0.0)
     fill(R("va", Z, Z + 1), 0.0)
     fill(R("vb", Z, Z + 1), 0.0)
-    tile_part("S", gl[2], 1280, Z)
-    tile_part("V", gl[2], 0, 480)
+    tile_part("S", gl[1], 1184, Z)
+    tile_part("V", gl[1], 0, 512)
     flush()
-    filler(99, 99)
-    tile_part("V", gl[2], 480, 1280)
-    cp("S", R("pn", 0, 1024), R("ps", PC, PC + 1024))
-    for bs in ((0, 1), (3, 4), (2,)):
-        q_mm(gl[2], bs)
-    for r in arrive:
-        mms(p_items(r, 1024, H, PC + 1024, 2 * N))
-    cp("V", R("qn", 0, 1024), R("ps", 0, 1024))
-    cp("S", R("qn", 1536, Z), R("ps", 1536, Z))
-    cp("V", R("qn", 1024, 1536), R("ps", 1024, 1536))
-    cp("S", R("pn", 1024, H), R("ps", PC + 1024, PC + H))
-
-    def swap(e, buf, c0, c1, h):
-        cp(e, R(buf, H + c0, H + c1, 64 * (1 - h), 64 * (2 - h)), R(buf, c0, c1, 64 * h, 64 * h + 64))
-
-    ndup = [0]
+    if NPRE >= 2:
+        double(EX + 256, 608)
+    sums_upto(gl[1], FIN[:2] if NPRE else FIN)
+    tile_part("V", gl[1], 512, 1184)
+    flush()
+    q_mm(gl[1])
+    for k in range(level[0], NPRE):
+        double(EX + 256, 608)
+    tile_part("S", gl[2], 1536, Z)
+    tile_part("V", gl[2], 0, 512)
+    flush()
+    sums_upto(gl[2], FIN)
+    tile_part("V", gl[2], 512, 1024)
+    tile_part("V", gl[2], 1024, 1536)
+    if arrive[-1] == data:
+        q_mm(gl[2])
+        sums_upto(data, FIN)
+    else:
+        for bs in ((0, 3, 4), (1,), (2,)):
+            q_mm(gl[2], bs)
+    plus("S", R("pn", 0, 1024), R("ps", PC, PC + 1024), LIFT)
+    plus("S", R("pn", 1024, H), R("ps", PC + 1024, PC + H), LIFT)
+    copies(crossed("pn", H - plan[0][0], H))
+    minus("V", R("qn", 0, 512), R("ps", 0, 512))
+    minus("S", R("qn", 1536, Z), R("ps", 1536, Z))
+    minus("V", R("qn", 512, 1536), R("ps", 512, 1536))
 
     def dup(e, buf, c0, c1):
         if e == "G":
             op("G", lambda: g.affine_select(T.vd[:, c0:c1], T[buf][:, c0:c1], [[0, c1 - c0]], A.is_ge, 0.0, 0, 0), [R(buf, c0, c1)], [R("vd", c0, c1)])
         else:
-            dmas("Y", "du%d" % ndup[0], [(T.vd[:, c0:c1], T[buf][:, c0:c1], [R(buf, c0, c1)], [R("vd", c0, c1)])])
-            ndup[0] += 1
+            copies([(R("vd", c0, c1), R(buf, c0, c1))])
 
-    def split(win, add, dst, lc, cuts, whole):
-        for i, (c0, c1) in enumerate(cuts):
-            gather("V", R(dst, c0, c1), R(win, 0, Z + 1), lc + c0 // 16, R(add, c0, c1))
-            dup("G", dst, c0, c1)
-            if i < 3:
-                swap("S", dst, c0, c1, 0)
-                swap("S", dst, c0, c1, 1)
-                if whole:
-                    dup("Y", dst, H + c0, H + c1)
-        swap("V", dst, c0, c1, 0)
-        swap("V", dst, c0, c1, 1)
-        if whole:
-            dup("Y", dst, H + c0, H + c1)
-
-    def mixed(win, dst, lc, x):
+    def one_round(win, add, dst, lc, now, nxt):
+        C, cuts, B = now
+        n = level[0]
+        ptr = n < 6
+        src, tb, lin, lout = tabs[n % 2], tabs[(n + 1) % 2], L0 + W * n, L0 + W * (n + 1)
         w = R(win, 0, Z + 1)
-        gather("V", R(dst, 0, x), w, lc, R("vd", 0, x))
-        dup("G", dst, 0, x)
-        gather("V", R(dst, x, H), w, lc + x // 16, R("vd", x, H))
-        dup("G", dst, x, 992)
-        dup("G", dst, 992, H)
+
+        def part(c0, c1):
+            gather("V", R(dst, c0, c1), w, lc + c0 // 16, R(add, c0, c1))
+        if ptr:
+            level[0] += 1
+            gather("S", R(tb, 0, B), R(src, 0, Z + 1), lin)
+        c = 0
+        for i, (k, who, twin) in enumerate(cuts):
+            part(c, c + k)
+            if who == "D":
+                copies(crossed(dst, c, c + k))
+            else:
+                for (o, x) in crossed(dst, c, c + k):
+                    cp("S", o, x)
+            dup(twin, dst, c, c + k)
+            c += k
+            if i == 0:
+                flush()
+                if ptr:
+                    gather("S", R(tb, B, H), R(src, 0, Z + 1), lin + B // 16)
+            if i == 1 and ptr:
+                if n < 5:
+                    copies(crossed(tb, 0, B), 1 if tb in fresh else 4)
+                extract(tb, 0, B, 0)
+        pend.extend(late)
+        del late[:]
+        if ptr:
+            pend.append((lout, B // 16, 0))
+        part(H - C, H)
+        dup("Y" if nxt[0] else "G", dst, H - C, H)
         flush()
-        swap("S", dst, x, H, 0)
-        swap("S", dst, x, H, 1)
-        gather("V", R(dst, H, H + x), w, lc + H // 16, R("vd", H, H + x))
+        if ptr:
+            if n < 5:
+                cs = [(B, H)] if H - B <= 512 else [(B, B + 512), (B + 512, H)]
+                mms([(R("ps", 1024 + c0 - B, 1024 + c1 - B), R("ex", 0, 128), R(tb, c0, c1), True, True) for (c0, c1) in cs])
+                cp("S", R(tb, H + B, Z), R("ps", 1024, 1024 + H - B))
+                if tb in fresh:
+                    fresh.remove(tb)
+            extract(tb, B, H, 512)
+            pend.append((lout + B // 16, (H - B) // 16, 512))
+            Cn = plan[n + 2][0]
+            if Cn:
+                extract(tb, H - Cn, H, 2048, "bc")
+                late.append((lout + (Z - Cn) // 16, Cn // 16, 2048))
+        part(Z - C, Z)
+        if nxt[0]:
+            dup("Y", dst, Z - nxt[0], Z)
 
-    X = H // 2
-    split("qn", "pn", "va", LI, [(0, 256), (256, 640), (640, 1024), (1024, H)], step_n[0] < 6)
     vs = ["va", "vb"]
+    one_round("qn", "pn", "va", LI, plan[0], plan[1])
+    again = [(at, c0, c1) for at in (PC, PD) for (c0, c1) in FIN]
     for b in range(6):
-        cur, nxt = vs[b % 2], vs[(b + 1) % 2]
-        lc = L0 + W * b
-        n = step_n[0]
-        src, dst, lin, lout = tabs[n % 2], tabs[(n + 1) % 2], L0 + W * n, L0 + W * (n + 1)
-        if n < 5:
-            def part(c0, c1):
-                gather("V", R(nxt, c0, c1), R(cur, 0, Z + 1), lc + c0 // 16, R("vd", c0, c1))
-                if n < 4 or c0 < H + X:
-                    dup("Y", nxt, c0, c1)
-            gather("S", R(dst, 0, H), R(src, 0, Z + 1), lin)
-            part(0, 512)
-            part(512, 1024)
-            flush()
-            gather("S", R(dst, H, Z), R(src, 0, Z + 1), lin + H // 16)
-            extract(dst, lout, 0)
-            part(1024, 1536)
-            part(1536, 2048)
-            part(2048, Z)
-            evac(lout, 0)
-            extract(dst, lout, 1)
-            pend.append((lout, 1))
-            step_n[0] += 1
-        elif n == 5:
-            gather("S", R(dst, 0, H), R(src, 0, Z + 1), lin)
-            mixed(cur, nxt, lc, X)
-            extract(dst, lout, 0)
-            pend.append((lout, 0))
-            step_n[0] += 1
-        else:
-            split(cur, "vd", nxt, lc, [(0, 256), (256, X), (X, 992), (992, H)], False)
-            flush()
-    flush()
+        one_round(vs[b % 2], "vd", vs[(b + 1) % 2], L0 + W * b, plan[b + 1], plan[b + 2])
+        while again and (b == 4 or len(again) > max(3, 5 - b) or level[0] == 6):
+            at, c0, c1 = again.pop(0)
+            mms([(R("ps", at + c0, at + c1), R("ef", 0, 128), R("pn", c0, c1), True, False)])
 
-    cur = vs[0]
     rid, pid, _ = topo.addr(T.cores[mate])
-    hh = H // 2
-    pc = [0, 1024]
-    qc = [2048, 3072]
 
-    def last(i):
-        gather("V", R("xf", i * hh, (i + 1) * hh), R(cur, 0, Z + 1), L0 + 6 * W + i * hh // 16, R("vd", i * hh, (i + 1) * hh))
+    def last(out, i):
+        c0, c1 = FIN[i]
+        gather("V", R(out, c0, c1), R(vs[0], 0, Z + 1), L0 + 6 * W + c0 // 16, R("vd", c0, c1))
 
-    def p_psum(i):
-        act(R("ps", pc[i], pc[i] + hh), R("pn", i * hh, (i + 1) * hh), F.Identity, bias=-127.5)
-
-    def sub_a(i):
-        c0, c1 = i * hh, (i + 1) * hh
-        tt(R("xj", c0, c1), R("ps", pc[i], pc[i] + hh), R("xf", c0, c1), A.subtract)
-
-    def res_a(out, i):
-        c0, c1 = i * hh, (i + 1) * hh
-        ts(R("xm", c0, c1), R("xj", c0, c1), 255, A.bitwise_and)
-        cp("V", R(out, c0, c1), R("xm", c0, c1))
-
-    def round_b(i):
-        c0, c1 = i * hh, (i + 1) * hh
-        act(R("xu", c0, c1), R("xf", c0, c1), F.Identity, bias=BIG)
-        act(R("ps", qc[i], qc[i] + hh), R("xu", c0, c1), F.Identity, bias=-BIG)
-
-    def rest_b(i):
-        c0, c1 = i * hh, (i + 1) * hh
-        tt(R("rb", c0, c1), R("xf", c0, c1), R("ps", qc[i], qc[i] + hh), A.subtract)
-
-    def res_b(out, i):
-        act(R(out, i * hh, (i + 1) * hh), R("rb", i * hh, (i + 1) * hh), F.Identity, bias=127.5)
+    def floor256(i):
+        c0, c1 = FIN[i]
+        act(R("xu", c0, c1), R("xf", c0, c1), bias=TOP - 128.0, scale=1.0 + 2.0 ** -20)
+        act(R("ps", c0, c1), R("xu", c0, c1), bias=-TOP)
 
     def hand(i):
-        c0, c1 = i * hh, (i + 1) * hh
+        c0, c1 = FIN[i]
         before("G", [R("osend", c0, c1)], [])
         g.remote_dma(T.oland[:, c0:c1], T.osend[:, c0:c1], T.sem["af%d" % i], T.sem.sent, pid, rid, bits(fin_e))
         sent[0] += len(fin_e)
+        mms([(R("ps", PC + c0, PC + c1), R("en", 0, 128), R("osend", c0, c1), False, True)])
+        mms([(R("ps", PD + c0, PD + c1), R("en", 0, 128), R("osend", c0, c1), False, False)])
+
+    def rest(i):
+        c0, c1 = FIN[i]
+        tt(R("osend", c0, c1), R("xf", c0, c1), R("ps", c0, c1), A.subtract)
+        hand(i)
+
+    def by_bits(i):
+        c0, c1 = FIN[i]
+        ts(R("xm", c0, c1), R("xj", c0, c1), 255, A.bitwise_and)
+        cp("V", R("osend", c0, c1), R("xm", c0, c1))
+        hand(i)
+
+    def keep_round(e, i):
+        c0, c1 = FIN[i]
+        plus(e, R("rb", c0, c1), R("ps", PC + c0, PC + c1), 49152.0 - 127.5)
+        mms([(R("ps", PD + c0, PD + c1), R("en", 0, 128), R("rb", c0, c1), False, True)])
 
     def store(e, sem, buf, rows, i):
-        c0, c1 = i * hh, (i + 1) * hh
+        c0, c1 = FIN[i]
         dmas(e, sem, [(T.y[64 * rows:64 * rows + 64, H * h + c0:H * h + c1], T[buf][64 * h:64 * h + 64, c0:c1],
                        [R(buf, c0, c1, 64 * h, 64 * h + 64)], []) for h in range(2)])
 
-    p_psum(0)
-    if s == 0:
-        last(0)
-        round_b(0)
-        last(1)
-        round_b(1)
-        rest_b(0)
-        ts(R("osend", 0, hh), R("rb", 0, hh), 127.5, A.add)
-        hand(0)
-        sub_a(0)
-        rest_b(1)
-        res_b("osend", 1)
-        hand(1)
-        p_psum(1)
-        res_a("okeep", 0)
-        store("S", "st0", "okeep", s, 0)
-        sub_a(1)
-        res_a("okeep", 1)
-        store("S", "st1", "okeep", s, 1)
-    else:
-        last(0)
-        round_b(0)
-        p_psum(1)
-        sub_a(0)
-        res_a("osend", 0)
-        hand(0)
-        last(1)
-        round_b(1)
-        sub_a(1)
-        res_a("osend", 1)
-        hand(1)
-        rest_b(0)
-        res_b("okeep", 0)
-        store("S", "st0", "okeep", s, 0)
-        rest_b(1)
-        ts(R("okeep", hh, H), R("rb", hh, H), 127.5, A.add)
-        store("S", "st1", "okeep", s, 1)
-    store("Y", "st2", "oland", 1 - s, 0)
-    store("Y", "st3", "oland", 1 - s, 1)
+    def keep(e, i):
+        c0, c1 = FIN[i]
+        plus(e, R("okeep", c0, c1), R("ps", PD + c0, PD + c1), 49152.0)
+        store("S", "st%d" % i, "okeep", s, i)
+
+    last("xf", 0)
+    floor256(0)
+    last("xf", 1)
+    floor256(1)
+    last("xj", 2)
+    rest(0)
+    by_bits(2)
+    rest(1)
+    keep_round("S", 0)
+    keep_round("V", 2)
+    keep_round("V", 1)
+    keep("S", 0)
+    keep("V", 2)
+    keep("V", 1)
+    for i in (0, 2, 1):
+        store("Y", "st%d" % (4 + i), "oland", 1 - s, i)
     cnt["sent"] = sent[0]
     for k in cnt:
         if cnt[k]:

@@ -4,18 +4,23 @@ from concourse.mybir import dt, AluOpType, AxisListType, ActivationFunctionType
 Z = 2560
 H = Z // 2
 W = Z // 16
-NPRE = 0
-NHELP = 2
-FIRST = 2
-EARLY = 1
-DIRECT = 0
-T0 = 1024
 ZS = Z + 16
+NHELP = 3
+ORDER = ("aonb", "aonb")
+SENDS = ("aAnbB", "aAnbB")
+CUT = ((0, 544, 1088, 1600), (0, 576, 1152, 1696))
+ARR = ("onab", "onab", "onab", "onab")
+FIRST = 2
+EARLY = 2
+PRE = (1, 1, 1, 1)
+NPRE = (0, 0)
+GZ = 768
+OWN, ZVS, T0, T1 = 640, (256, 640), 1024, 896
 TOP = 2147483648.0
 LIFT = 1536.0
-ROUND_PTR = (512, [(256, "D", "G"), (256, "D", "G"), (256, "S", "G")], 512)
-ROUND_END = (384, [(256, "D", "G"), (256, "D", "G"), (384, "S", "G")], 512)
-ROUND_FREE = (288, [(224, "S", "G"), (384, "S", "G"), (384, "S", "G")], 0)
+ROUND_PTR = (448, [(352, "D", ""), (224, "D", "G"), (256, "S", "")], 704, "FP")
+ROUND_END = (448, [(352, "D", ""), (224, "D", "G"), (256, "S", "")], 704, "F")
+ROUND_FREE = (384, [(192, "S", "G"), (352, "S", "G"), (352, "S", "G")], 0, "")
 FIN = [(0, 512), (512, 1024), (1024, H)]
 
 SCRATCH = {
@@ -29,7 +34,8 @@ SCRATCH = {
     "zeroi": ("sbuf", [128, W], "int32"),
     "zb": ("sbuf", [128, W], "bfloat16"),
     "zf": ("sbuf", [128, 2 * W], "float32"),
-    "ci": ("sbuf", [128, 8], "int32"),
+    "ci": ("sbuf", [128, 16], "int32"),
+    "vz": ("sbuf", [128, 128], "bfloat16"),
     "cf": ("sbuf", [128, 64], "float32"),
     "mk": ("sbuf", [128, 80], "float32"),
     "row": ("sbuf", [128, 176], "float32"),
@@ -68,7 +74,7 @@ SEMAPHORES = (["eV", "eS", "eP", "eG", "sent", "api", "lpi", "llo", "lze", "go",
               + ["at%d" % i for i in range(4)] + ["af%d" % i for i in range(4)] + ["st%d" % i for i in range(8)] + ["du%d" % i for i in range(70)])
 
 LA, LB, LI, L0, LQ, LZ = 0, W, 2 * W, 3 * W, 10 * W, 13 * W
-EX = 3584
+EX = 2048
 PC = 2560
 PD = 1024
 TAB = {"pib": 0, "ta": ZS, "tb": 2 * ZS}
@@ -93,16 +99,14 @@ def helpers(q, T, topo):
 
 def tile_order(q, T, topo):
     off, on = send_order(q, T, topo)
-    if on == [len(T.cores) - 1]:
-        return [off[0], on[0], off[1], q]
-    return off + on + [q]
+    names = {"a": off[0], "b": off[1], "n": on[0], "o": q}
+    return [names[c] for c in ORDER[q % 2]]
 
 
 def expected(r, q, T, topo):
     off, on = send_order(r, T, topo)
-    if q in off:
-        return 14 + 3 * off.index(q)
-    return 12 if (q == r) == (q == len(T.cores) - 1) else 11
+    names = {"a": off[0], "b": off[1], "n": on[0], "o": r}
+    return [names[c] for c in ARR[q]].index(q)
 
 
 def bits(engines):
@@ -130,15 +134,21 @@ def small_engines(q, T, topo):
         small[d] = pow2(e[i * n:(i + 1) * n])
     for i, d in enumerate(on):
         e = [k for k in topo.engines(me, T.cores[d]) if k not in used]
-        n = len(e) // len(on)
-        small[d] = pow2(e[i * n:(i + 1) * n])
+        n = len(small[off[0]])
+        small[d] = e[i * n:(i + 1) * n]
     return small
 
 
-def hop_engines(q, i, T, topo):
-    e = topo.engines(T.cores[q], helpers(q, T, topo)[i])
-    n = len(e) // NHELP
-    return e[i * n:(i + 1) * n]
+def near_engines(q, T, topo):
+    return topo.engines(T.cores[q], T.cores[send_order(q, T, topo)[1][0]])
+
+
+def hop_engines(q, k, i, T, topo):
+    e = near_engines(q, T, topo)
+    if CUT[k][-1] < Z:
+        far = topo.engines(T.cores[q], T.cores[send_order(q, T, topo)[0][k]])
+        return pow2([x for x in e if x not in far])
+    return e
 
 
 def helper_program(g, core, T, topo):
@@ -146,14 +156,12 @@ def helper_program(g, core, T, topo):
         hs = helpers(q, T, topo)
         if core in hs:
             i = hs.index(core)
-            w = Z // NHELP
             n = 0
             for k, d in enumerate(send_order(q, T, topo)[0]):
-                if k < DIRECT:
-                    continue
-                g.wait_ge(T.sem["hop%d" % k], len(hop_engines(q, i, T, topo)))
+                c0, c1 = CUT[k][i], CUT[k][i + 1]
+                g.wait_ge(T.sem["hop%d" % k], len(hop_engines(q, k, i, T, topo)))
                 rid, pid, _ = topo.addr(T.cores[d])
-                g.remote_dma(T.xt[:, q * Z + i * w:q * Z + (i + 1) * w], T.xs[:, k * w:(k + 1) * w], T.sem["at%d" % q], T.sem.sent,
+                g.remote_dma(T.xt[:, q * Z + c0:q * Z + c1], T.xs[:, k * Z + c0:k * Z + c1], T.sem["at%d" % q], T.sem.sent,
                              pid, rid, topo.mask(core, T.cores[d]))
                 n += len(topo.engines(core, T.cores[d]))
             if n:
@@ -316,8 +324,12 @@ def rank_program(g, core, T, topo):
             [R("pih", r * W, (r + 1) * W) for r in range(data) if r != q])
     for r in range(N):
         if r != q:
-            via = [T.cores[r]] if r in on or send_order(r, T, topo)[0].index(q) < DIRECT else helpers(r, T, topo)
-            landing("at%d" % r, sum(len(topo.engines(c, core)) for c in via), [R("xt", r * Z, (r + 1) * Z)])
+            if r in on:
+                n = len(near_engines(r, T, topo))
+            else:
+                own = [T.cores[r]] if CUT[send_order(r, T, topo)[0].index(q)][-1] < Z else []
+                n = sum(len(topo.engines(c, core)) for c in helpers(r, T, topo) + own)
+            landing("at%d" % r, n, [R("xt", r * Z, (r + 1) * Z)])
     mate = q ^ 1
     fin_e = topo.engines(core, T.cores[mate])
     for i, (c0, c1) in enumerate(FIN):
@@ -336,7 +348,7 @@ def rank_program(g, core, T, topo):
         dmas("S", "lpi", its[2:])
         after("D", [], [R("pis", 0, 4 * W)], ("lpi", cnt["lpi"]))
     dmas("S", "llo", [(T.losti[64 * t:64 * t + 64, 0:2], T.lost[64 * s:64 * s + 64, :], [], [R("losti", 0, 2, 64 * t, 64 * t + 64)]) for t in range(2)])
-    dmas("S", "lze", [(T.zeroi[64 * t:64 * t + 64, :], T.zero[64 * s:64 * s + 64, :], [], [R("zeroi", 0, W, 64 * t, 64 * t + 64)]) for t in range(1 + s)])
+    dmas("Y", "lze", [(T.zeroi[64 * t:64 * t + 64, :], T.zero[64 * s:64 * s + 64, :], [], [R("zeroi", 0, W, 64 * t, 64 * t + 64)]) for t in range(1 + s)])
     seq = tile_order(q, T, topo)
     sent = [0]
 
@@ -346,49 +358,61 @@ def rank_program(g, core, T, topo):
         dmas("Y", "lx%d" % d, [(T[buf][64 * t:64 * t + 64, c:c + Z], T.x[64 * ds:64 * ds + 64, (2 * t + dz) * Z:(2 * t + dz + 1) * Z],
                                 [], [R(buf, c, c + Z, 64 * t, 64 * t + 64)]) for t in range(2)])
 
-    def send(d):
-        c = slot[d] * Z
-        before("G", [R("xs", c, c + Z)], [])
-        if d in on or off.index(d) < DIRECT:
+    def send(c):
+        k = "ab".find(c.lower())
+        d = off[k] if k >= 0 else on[0]
+        at = slot[d] * Z
+        before("G", [R("xs", at, at + Z)], [])
+        if c.islower():
+            c0 = CUT[k][-1] if k >= 0 else 0
+            e = topo.engines(core, T.cores[d])
             rid, pid, _ = topo.addr(T.cores[d])
-            g.remote_dma(T.xt[:, q * Z:(q + 1) * Z], T.xs[:, c:c + Z], T.sem["at%d" % q], T.sem.sent, pid, rid, topo.mask(core, T.cores[d]))
-            sent[0] += len(topo.engines(core, T.cores[d]))
+            g.remote_dma(T.xt[:, q * Z + c0:(q + 1) * Z], T.xs[:, at + c0:at + Z], T.sem["at%d" % q], T.sem.sent, pid, rid, bits(e))
+            sent[0] += len(e)
             return
-        trs, w, k = [], Z // NHELP, off.index(d)
+        trs = []
         for i, hc in enumerate(helpers(q, T, topo)):
             rid, pid, _ = topo.addr(hc)
-            e = hop_engines(q, i, T, topo)
+            c0, c1 = CUT[k][i], CUT[k][i + 1]
+            e = hop_engines(q, k, i, T, topo)
             trs.append(RemoteDMATransfer(dst_ids=[DstId(rid=rid, pnc=pid)], dma_engine_mask=bits(e), remote_sem=T.sem["hop%d" % k],
-                                         src=T.xs[:, c + i * w:c + (i + 1) * w], dst=T.xs[:, k * w:(k + 1) * w]))
+                                         src=T.xs[:, at + c0:at + c1], dst=T.xs[:, k * Z + c0:k * Z + c1]))
             sent[0] += len(e)
-        g.remote_dma_fused(trs, local_sem=T.sem.sent)
+        for t in trs:
+            g.remote_dma_fused([t], local_sem=T.sem.sent)
 
     for d in seq[:FIRST]:
         load(d)
-    op("G", lambda: g.iota(T.ci[:, 0:1], [[0, 1]], 0, 1), [], [R("ci", 0, 1)])
+    op("G", lambda: g.iota(T.ci[:, 0:2], [[64, 2]], 0, 1), [], [R("ci", 0, 2)])
     op("G", lambda: g.iota(T.row[:], [[1, 176]], -16, 0, allow_small_or_imprecise_dtypes=True), [], [R("row", 0, 176)])
+    op("G", lambda: g.iota(T.inv[:, 0:GZ], [[0, GZ]], 0, 0, allow_small_or_imprecise_dtypes=True), [], [R("inv", 0, GZ)])
 
     EQ = 32
-    fill(R("inv", 0, H), 0.0)
-    p = R("ci", 0, 1)
-    ts(R("ci", 4, 5), p, 15, A.bitwise_and)
-    ts(R("ci", 5, 6), p, 6, A.arith_shift_right)
-    ts(R("ci", 1, 2), p, 63, A.bitwise_and)
-    ts(R("ci", 2, 3), p, 48, A.bitwise_and)
-    ts(R("ci", 3, 4), p, 112, A.bitwise_and)
     fill(R("eb", 0, 256), 0.0)
-    cp("V", col(1, 5), R("ci", 1, 6))
-    cp("V", col(54), p)
+    p, p2 = R("ci", 0, 1), R("ci", 0, 2)
+    ts(R("ci", 2, 3), p, 15, A.bitwise_and)
+    ts(R("ci", 3, 4), p, 6, A.arith_shift_right)
+    ts(R("ci", 4, 5), p, 63, A.bitwise_and)
+    cp("V", col(4, 2), R("ci", 2, 4))
+    ts(R("ci", 5, 6), p, 48, A.bitwise_and)
     ts(col(EQ, 16), R("row", 16, 32), col(4), A.is_equal)
-    ts(col(15, 3), R("row", 16, 22, step=2), col(5), A.add)
+    ts(R("ci", 6, 8), p2, 112, A.bitwise_and)
     ts(col(6), col(EQ), col(EQ + 1), A.add, col(EQ + 4), A.add)
     ts(col(8), col(EQ + 1), col(5), A.mult, col(EQ + 4), A.add)
-    ts(col(7), col(EQ), col(EQ + 4), A.subtract)
     ts(R("mk", 0, 65), R("row", 16, 81), col(6), A.mult)
     ts(col(9), col(8), 20.0, A.mult)
+    ts(R("ci", 8, 10), p2, 127, A.bitwise_and)
+    ts(R("ci", 10, 12), p2, 4, A.arith_shift_right, 4, A.bitwise_and)
+    ts(col(15, 3), R("row", 16, 22, step=2), col(5), A.add)
+    cp("V", col(56, 8), R("ci", 4, 12))
+    ts(col(10), col(EQ), col(EQ + 4), A.subtract, 20.0, A.mult)
+    ts(col(49), col(EQ + 1), 64.0, A.mult, col(EQ + 8), A.add)
     if q < data:
-        ts(R("pio", 0, 4 * W), R("pis", 0, 4 * W), -1280.0, A.add)
-        before("G", [R("pio", 0, 4 * W)], [])
+        mine = (2 * s + z) * W
+        parts = [(c0, c1) for (c0, c1) in ((0, mine), (mine + W, 4 * W)) if c0 < c1]
+        for (c0, c1) in parts + [(mine, mine + W)]:
+            ts(R("pio", c0, c1), R("pis", c0, c1), -1280.0, A.add)
+        before("G", [R("pio", c0, c1) for (c0, c1) in parts], [])
         trs = []
         for d in order:
             rid, pid, _ = topo.addr(T.cores[d])
@@ -397,69 +421,73 @@ def rank_program(g, core, T, topo):
                                          src=T.pio[:, b * W:(b + 1) * W], dst=T.pih[:, q * W:(q + 1) * W]))
             sent[0] += len(small_e[d])
         g.remote_dma_fused(trs, local_sem=T.sem.sent)
-    for d in seq[:EARLY]:
-        send(d)
+    for c in SENDS[s][:EARLY]:
+        send(c)
     if FIRST < N:
         g.sem_inc(T.sem.go, 1)
         g.sync.wait_ge(T.sem.go, 1)
     for d in seq[FIRST:]:
         load(d)
-    for d in seq[EARLY:]:
-        if d != q:
-            send(d)
+    for c in SENDS[s][EARLY:]:
+        send(c)
 
+    for buf in ("qn", "va", "vb"):
+        op("G", lambda buf=buf: g.iota(T[buf][:, Z:Z + 1], [[0, 1]], 0, 0, allow_small_or_imprecise_dtypes=True), [], [R(buf, Z, Z + 1)])
+    op("G", lambda: g.iota(T.vz[:], [[0, 128]], 0, 0, allow_small_or_imprecise_dtypes=True), [], [R("vz", 0, 128)])
     act(R("iw", 0, 64), R("row", 16, 80), bias=col(9), scale=col(EQ + 8))
-    act(col(10), col(7), scale=20.0)
     act(col(12), col(5), bias=1.0, scale=-1.0)
+    if s == 1:
+        act(R("zf", 0, W), R("row", 16, 16 + W), bias=col(4), scale=16.0)
     for k in range(1, 4):
         act(R("iw", 64 * k, 64 * k + 64), R("iw", 0, 64), bias=R("mk", k, k + 1))
     for k in range(1, 5):
         act(R("iw", 256 * k, 256 * k + 256), R("iw", 0, 256), bias=R("mk", 4 * k, 4 * k + 1))
-    cp("V", col(13, 2), R("losti", 0, 2))
-    ts(R("eb", 64, 128), R("row", 16, 80), col(1), A.is_equal)
-    ts(R("eb", 128, 192), R("row", 16, 80), col(1), A.is_equal)
-    ts(col(18, 3), col(15, 3), col(13 + s), A.is_equal)
-    ts(col(21, 3), col(15, 3), col(14 - s), A.is_equal)
-    if s == 1:
-        cp("V", R("iw", Z, Z + 1), R("mk", 64, 65))
-        ts(R("zf", 0, W), R("row", 16, 16 + W), 16.0, A.mult, col(4), A.add)
-    tt(col(24, 3), col(18, 3), col(21, 3), A.add)
-    if s == 1:
-        ts(R("zf", W, 2 * W), R("zeroi", 0, W), float(Z), A.mult)
-    ts(col(27, 3), col(24, 3), -1.0, A.add)
-    if s == 1:
-        tt(R("zf", 0, W), R("zf", 0, W), R("zf", W, 2 * W), A.max)
-    ts(R("iw", H, Z), R("iw", 0, H), col(10), A.add)
-    for r in range(N):
-        act(R("wp", 256 * r, 256 * r + 256), R("eb", 0, 256), scale=col(27 + r if r < data else 12))
-    if s == 1:
-        cp("V", R("lst", LZ, LZ + W), R("zf", 0, W))
-        gather("S", R("iz", 960, Z), R("iw", 0, Z + 1), LZ + 60)
-    for r in range(data):
-        ts(R("sa", 256 * r, 256 * r + 256), R("eb", 0, 256), col(18 + r), A.mult)
-    for r in range(data):
-        ts(R("sb", 128 * r, 128 * r + 128), R("eb", 64, 192), col(21 + r), A.mult)
-    fill(R("inv", H, Z), 0.0)
-    if s == 1:
-        gather("V", R("iz", 0, 960), R("iw", 0, Z + 1), LZ)
-    act(R("wq", 0, 128), R("eb", 64, 192), scale=col(5))
-    act(col(48, 5), col(EQ, 5), bias=col(EQ + 8), scale=64.0)
-    act(col(56), col(7), scale=col(5))
-    act(col(53), col(5), bias=col(3), scale=-128.0)
-    act(col(55), col(5), bias=col(54), scale=-128.0)
-    act(col(30), col(56), bias=col(48), scale=-64.0)
-    act(col(31), col(56), bias=col(52), scale=64.0)
-    act(col(53), col(53), bias=64.0)
-    act(col(55), col(55), bias=64.0)
 
     def q_list(r):
         ts(R("lst", LQ + r * W, LQ + (r + 1) * W), pi_of(r, 0, W), 1280.0, A.add)
-    if q < data:
+
+    def tile_part(e, r, c0, c1):
+        gather(e, R("gq", r * Z + c0, r * Z + c1), R("xt", r * Z, (r + 1) * Z), LQ + r * W + c0 // 16)
+    ZV = ZVS[q == data]
+    early = int(s == 0 and q in seq[:FIRST])
+    act(R("iw", H, Z), R("iw", 0, H), bias=col(10))
+    if s == 1:
+        ts(R("zf", W, 2 * W), R("zeroi", 0, W), float(Z), A.mult)
+        cp("V", R("iw", Z, Z + 1), R("mk", 64, 65))
+    else:
         q_list(q)
+    cp("V", col(13, 2), R("losti", 0, 2))
+    if s == 1:
+        tt(R("zf", 0, W), R("zf", 0, W), R("zf", W, 2 * W), A.max)
+    ts(R("eb", 64, 128), R("row", 16, 80), col(56), A.is_equal)
+    ts(R("eb", 128, 192), R("row", 16, 80), col(56), A.is_equal)
+    if s == 1:
+        cp("V", R("lst", LZ, LZ + W), R("zf", 0, W))
+        gather("S", R("iz", ZV, Z), R("iw", 0, Z + 1), LZ + ZV // 16)
+    elif early:
+        tile_part("S", q, OWN, Z)
+    ts(col(18, 3), col(15, 3), col(13 + s), A.is_equal)
+    ts(col(21, 3), col(15, 3), col(14 - s), A.is_equal)
     if s == 0:
         ts(R("zb", 0, W, 0, 64), R("zeroi", 0, W, 0, 64), 4096.0, A.mult)
-    ts(R("by", 0, 80), R("row", 0, 80), col(2), A.is_equal, col(49), A.mult)
-    ts(R("by", 80, 144), R("row", 16, 80), col(2), A.is_equal, col(49), A.mult)
+    for r in range(data):
+        ts(R("sa", 256 * r, 256 * r + 256), R("eb", 0, 256), col(18 + r), A.mult)
+    tt(col(24, 3), col(18, 3), col(21, 3), A.add)
+    for r in range(data):
+        ts(R("sb", 128 * r, 128 * r + 128), R("eb", 64, 192), col(21 + r), A.mult)
+    ts(col(27, 3), col(24, 3), -1.0, A.add)
+    if s == 1 and q < data:
+        q_list(q)
+    fill(R("inv", GZ, Z), 0.0)
+    for r in range(N):
+        ts(R("wp", 256 * r, 256 * r + 256), R("eb", 0, 256), col(27 + r if r < data else 12), A.mult)
+    ts(R("wq", 0, 128), R("eb", 64, 192), col(5), A.mult)
+    ts(R("by", 0, 80), R("row", 0, 80), col(57), A.is_equal, col(49), A.mult)
+    ts(R("by", 80, 144), R("row", 16, 80), col(57), A.is_equal, col(49), A.mult)
+    if early:
+        tile_part("V", q, 0, OWN)
+    if s == 1:
+        gather("V", R("iz", 0, ZV), R("iw", 0, Z + 1), LZ)
 
     arrive = sorted(range(N), key=lambda r: expected(r, q, T, topo))
     gl = [r for r in arrive if r < data]
@@ -494,20 +522,21 @@ def rank_program(g, core, T, topo):
                 mms([(R("ps", PC + c0, PC + c1), R("wp", 256 * r + 128 * (1 - h), 256 * r + 128 * (2 - h)),
                       R("xt", r * Z + H * h + c0, r * Z + H * h + c1)) + flags(("p", c0), 2 * N) for h in range(2)])
 
-    def sums_upto(r, chunks):
-        for x in arrive[:arrive.index(r) + 1]:
-            p_mm(x, chunks)
-            if x == data and (x, -1) not in emitted:
-                emitted.append((x, -1))
-                for bs in ((0, 3), (1, 4), (2,)):
-                    q_mm(x, bs)
+    def sums(r, banks):
+        if len(banks) > 3:
+            p_mm(r, FIN)
+        if r == data:
+            todo = [b for b in banks if (r, -1 - b) not in emitted]
+            emitted.extend((r, -1 - b) for b in todo)
+            for i in range(0, len(todo), 2):
+                q_mm(r, todo[i:i + 2])
 
-    plan = [ROUND_PTR if NPRE + i < 5 else ROUND_END if NPRE + i == 5 else ROUND_FREE for i in range(7)] + [(0, [], 0)]
+    plan = [ROUND_PTR] * (5 - NPRE[s]) + [ROUND_END] + [ROUND_FREE] * (1 + NPRE[s]) + [(0, [], 0, "")]
 
     def extract(tab, c0, c1, at, mat="bx"):
         mms([(R("ps", at, at + (c1 - c0) // 16), R(mat, 16 - r, 144 - r), R(tab, c0 + r, c1, step=16), r == 0, r == 15) for r in range(16)])
 
-    pend, late = [], []
+    pend, late, cross = [], [], []
 
     def flush():
         while pend:
@@ -531,69 +560,79 @@ def rank_program(g, core, T, topo):
             fresh.remove(dst)
         extract(dst, 0, H, at)
         pend.append((lout, 80, at))
-        C = plan[n + 2][0]
-        extract(dst, H - C, H, at + 80, "bc")
-        pend.append((lout + (Z - C) // 16, C // 16, at + 80))
+        cross.append((dst, lout, plan[n + 2][0]))
 
-    def tile_part(e, r, c0, c1):
-        gather(e, R("gq", r * Z + c0, r * Z + c1), R("xt", r * Z, (r + 1) * Z), LQ + r * W + c0 // 16)
-
-    p_mm(arrive[0], FIN[:2])
+    gs = gl[early:]
+    if early:
+        q_mm(q, range(4))
+    for r in arrive[:PRE[q]]:
+        sums(r, range(4))
     mms([(R("ps", EX, EX + W), R("by", 16 - r, 144 - r), R("inv", r, Z, step=16), r == 0, r == 15 and s == 1) for r in range(16)])
     if s == 0:
         mms([(R("ps", EX, EX + W), R("eb", 64, 192, 0, 64), R("zb", 0, W, 0, 64), False, True)])
-    ts(R("tab", Z, 3 * ZS, step=ZS), R("row", 0, 3), 0.0, A.mult, R("mk", 64, 65), A.add)
-    ts(R("bx", 0, 144), R("row", 0, 144), col(3), A.is_equal, col(30), A.mult)
-    ts(R("bc", 0, 144), R("row", 0, 144), col(53), A.is_equal, col(31), A.mult)
-    tile_part("S", gl[0], T0, Z)
-    tile_part("V", gl[0], 0, 480)
-    for c in (0, 80):
-        for h in range(2):
-            ts(R("lst", LI + c, LI + c + 80, 64 * h, 64 * h + 64), R("ps", EX + (c + 80 * h) % W, EX + (c + 80 * h) % W + 80, 64 * h, 64 * h + 64),
-               float(Z), A.min)
-    sums_upto(arrive[1], FIN[:2])
-    double(EX + 256, 576)
-    mid = (480 + T0) // 64 * 32
-    tile_part("S", gl[0], mid, T0)
-    tile_part("V", gl[0], 480, mid)
     for r in gl[1:]:
-        q_list(r)
-    q_mm(gl[0])
-    ts(R("ex", 0, 128), R("row", 16, 144), col(55), A.is_equal)
-    ts(R("en", 0, 128), R("row", 16, 144), col(54), A.is_equal, -1.0, A.mult)
-    ts(R("ef", 0, 128), R("row", 16, 144), col(54), A.is_equal)
-    fill(R("qn", Z, Z + 1), 0.0)
-    fill(R("va", Z, Z + 1), 0.0)
-    fill(R("vb", Z, Z + 1), 0.0)
-    tile_part("S", gl[1], 1184, Z)
-    tile_part("V", gl[1], 0, 512)
+        if r != q:
+            q_list(r)
+    tile_part("S", gs[0], T0, Z)
+    ts(col(28 + 22, 2), col(62, 2), col(4), A.is_equal, 64.0, A.mult)
+    ts(R("tab", Z, 3 * ZS, step=ZS), R("row", 0, 3), 0.0, A.mult, R("mk", 64, 65), A.add)
+    ts(col(30, 2), col(50, 2), col(EQ + 8), A.add)
+    ts(R("ex", 0, 128), R("row", 16, 144), col(61), A.is_equal)
+    ts(R("bx", 0, 144), R("row", 0, 144), col(58), A.is_equal, col(30), A.mult)
+    ts(R("bc", 0, 144), R("row", 0, 144), col(59), A.is_equal, col(31), A.mult)
+    ts(R("ef", 0, 128), R("row", 16, 144), col(60), A.is_equal)
+    for (c0, c1, at, h) in ((0, 80, 80, 1), (0, W, 0, 0), (80, W, 0, 1)):
+        ts(R("lst", LI + c0, LI + c1, 64 * h, 64 * h + 64), R("ps", EX + at, EX + at + c1 - c0, 64 * h, 64 * h + 64), float(Z), A.min)
+    sums(arrive[PRE[q]], range(4))
+    q_mm(gs[0], (2, 3))
+    double(EX + 256, 608)
+    sums(arrive[PRE[q] + 1], range(4))
+    tile_part("V", gs[0], 0, T0)
+    if not early:
+        tile_part("S", gs[1], 1536, Z)
     flush()
-    if NPRE >= 2:
-        double(EX + 256, 608)
-    sums_upto(gl[1], FIN[:2] if NPRE else FIN)
-    tile_part("V", gl[1], 512, 1184)
-    flush()
-    q_mm(gl[1])
-    for k in range(level[0], NPRE):
+    q_mm(gs[0], (0, 1))
+    if not early:
+        tile_part("S", gs[1], T1, 1536)
+        tile_part("V", gs[1], 0, T1)
+    for k in range(NPRE[s]):
         double(EX + 256, 608)
     tile_part("S", gl[2], 1536, Z)
     tile_part("V", gl[2], 0, 512)
     flush()
-    sums_upto(gl[2], FIN)
     tile_part("V", gl[2], 512, 1024)
     tile_part("V", gl[2], 1024, 1536)
-    if arrive[-1] == data:
-        q_mm(gl[2])
-        sums_upto(data, FIN)
-    else:
-        for bs in ((0, 3, 4), (1,), (2,)):
-            q_mm(gl[2], bs)
+    if early:
+        q_mm(q, (4,))
+    q_mm(gs[0], (4,))
+    if not early:
+        q_mm(gs[1], (3, 4))
+    for r in arrive[:-1]:
+        sums(r, range(5))
+    if not early:
+        q_mm(gs[1], (0, 1, 2))
+    p_mm(arrive[-1], FIN[:2])
     plus("S", R("pn", 0, 1024), R("ps", PC, PC + 1024), LIFT)
-    plus("S", R("pn", 1024, H), R("ps", PC + 1024, PC + H), LIFT)
-    copies(crossed("pn", H - plan[0][0], H))
+    q_mm(gl[2], (0,))
+    sums(data, (0, 3, 4))
+    q_mm(gl[2], (3, 4))
+    sums(data, (1, 2))
+    q_mm(gl[2], (1,))
+    q_mm(gl[2], (2,))
+    p_mm(arrive[-1], FIN)
     minus("V", R("qn", 0, 512), R("ps", 0, 512))
     minus("S", R("qn", 1536, Z), R("ps", 1536, Z))
-    minus("V", R("qn", 512, 1536), R("ps", 512, 1536))
+    minus("V", R("qn", 512, 1024), R("ps", 512, 1024))
+    minus("V", R("qn", 1024, 1536), R("ps", 1024, 1536))
+    plus("S", R("pn", 1024, H), R("ps", PC + 1024, PC + H), LIFT)
+    copies(crossed("pn", H - plan[0][0], H))
+    for i, (dst, lout, C) in enumerate(cross):
+        if i + 1 < len(cross):
+            extract(dst, H - C, H, 2048 + 64 * i, "bc")
+            pend.append((lout + (Z - C) // 16, C // 16, 2048 + 64 * i))
+        else:
+            extract(dst, H - C, H, 128 - C // 16, "bc")
+            late.append(C // 16)
 
     def dup(e, buf, c0, c1):
         if e == "G":
@@ -602,18 +641,33 @@ def rank_program(g, core, T, topo):
             copies([(R("vd", c0, c1), R(buf, c0, c1))])
 
     def one_round(win, add, dst, lc, now, nxt):
-        C, cuts, B = now
+        C, cuts, B, when = now
         n = level[0]
-        ptr = n < 6
         src, tb, lin, lout = tabs[n % 2], tabs[(n + 1) % 2], L0 + W * n, L0 + W * (n + 1)
         w = R(win, 0, Z + 1)
 
         def part(c0, c1):
             gather("V", R(dst, c0, c1), w, lc + c0 // 16, R(add, c0, c1))
-        if ptr:
+
+        def jump(c0, c1):
+            gather("S", R(tb, c0, c1), R(src, 0, Z + 1), lin + c0 // 16)
+
+        def over(c0, c1):
+            if n < 5:
+                copies(crossed(tb, c0, c1), 1 if tb in fresh else 4)
+
+        def second():
+            extract(tb, B, H, 512)
+            pend.append((lout + B // 16, (H - B) // 16, 512))
+            if n < 5:
+                Cn = plan[n + 2][0]
+                extract(tb, H - Cn, H, 128 - Cn // 16, "bc")
+                late.append(Cn // 16)
+        if when:
             level[0] += 1
-            gather("S", R(tb, 0, B), R(src, 0, Z + 1), lin)
-        c = 0
+        if "F" in when:
+            jump(0, B)
+        c = done = 0
         for i, (k, who, twin) in enumerate(cuts):
             part(c, c + k)
             if who == "D":
@@ -621,48 +675,45 @@ def rank_program(g, core, T, topo):
             else:
                 for (o, x) in crossed(dst, c, c + k):
                     cp("S", o, x)
-            dup(twin, dst, c, c + k)
             c += k
-            if i == 0:
+            if twin:
+                dup(twin, dst, done, c)
+                done = c
+            if i == 1:
                 flush()
-                if ptr:
-                    gather("S", R(tb, B, H), R(src, 0, Z + 1), lin + B // 16)
-            if i == 1 and ptr:
-                if n < 5:
-                    copies(crossed(tb, 0, B), 1 if tb in fresh else 4)
-                extract(tb, 0, B, 0)
-        pend.extend(late)
-        del late[:]
-        if ptr:
-            pend.append((lout, B // 16, 0))
+                if "F" in when:
+                    jump(B, H)
+            if i == 1 and "F" in when:
+                over(0, B)
+                extract(tb, 0, B, 128)
+        if when:
+            k = late.pop() if late else 0
+            pend.append((lout - k, k + B // 16, 128 - k))
         part(H - C, H)
-        dup("Y" if nxt[0] else "G", dst, H - C, H)
-        flush()
-        if ptr:
-            if n < 5:
-                cs = [(B, H)] if H - B <= 512 else [(B, B + 512), (B + 512, H)]
-                mms([(R("ps", 1024 + c0 - B, 1024 + c1 - B), R("ex", 0, 128), R(tb, c0, c1), True, True) for (c0, c1) in cs])
-                cp("S", R(tb, H + B, Z), R("ps", 1024, 1024 + H - B))
-                if tb in fresh:
-                    fresh.remove(tb)
-            extract(tb, B, H, 512)
-            pend.append((lout + B // 16, (H - B) // 16, 512))
-            Cn = plan[n + 2][0]
-            if Cn:
-                extract(tb, H - Cn, H, 2048, "bc")
-                late.append((lout + (Z - Cn) // 16, Cn // 16, 2048))
+        dup("G", dst, done, H)
         part(Z - C, Z)
         if nxt[0]:
             dup("Y", dst, Z - nxt[0], Z)
+        flush()
+        if "P" in when:
+            cs = [(B, H)] if H - B <= 512 else [(B, B + 512), (B + 512, H)]
+            mms([(R("ps", 1024 + c0 - B, 1024 + c1 - B), R("ex", 0, 128), R(tb, c0, c1), True, True) for (c0, c1) in cs])
+            cp("S", R(tb, H + B, Z), R("ps", 1024, 1024 + H - B))
+        if "F" in when:
+            second()
+        if when and tb in fresh:
+            fresh.remove(tb)
 
     vs = ["va", "vb"]
+    op("G", lambda: g.affine_select(T.en[:], T.vz[:, 0:128], [[-1, 128]], A.not_equal, -1.0, 0, 1), [R("vz", 0, 128)], [R("en", 0, 128)])
     one_round("qn", "pn", "va", LI, plan[0], plan[1])
     again = [(at, c0, c1) for at in (PC, PD) for (c0, c1) in FIN]
     for b in range(6):
         one_round(vs[b % 2], "vd", vs[(b + 1) % 2], L0 + W * b, plan[b + 1], plan[b + 2])
-        while again and (b == 4 or len(again) > max(3, 5 - b) or level[0] == 6):
+        while again and (b == 4 or len(again) > max(3, 5 - b)):
             at, c0, c1 = again.pop(0)
             mms([(R("ps", at + c0, at + c1), R("ef", 0, 128), R("pn", c0, c1), True, False)])
+    flush()
 
     rid, pid, _ = topo.addr(T.cores[mate])
 

from concourse.bass import DstId, RemoteDMATransfer
from concourse.mybir import dt, AluOpType, AxisListType, ActivationFunctionType

Z = 2560
H = Z // 2
W = Z // 16
ZS = Z + 16
NHELP = 3
ORDER = ("aonb", "aonb")
SENDS = ("aAnbB", "aAnbB")
CUT = ((0, 544, 1088, 1600), (0, 576, 1152, 1696))
ARR = ("onab", "onab", "onab", "onab")
FIRST = 2
EARLY = 2
PRE = (1, 1, 1, 1)
NPRE = (0, 0)
GZ = 768
OWN, ZVS, T0, T1 = 640, (256, 640), 1024, 896
TOP = 2147483648.0
LIFT = 1536.0
ROUND_PTR = (448, [(352, "D", ""), (224, "D", "G"), (256, "S", "")], 704, "FP")
ROUND_END = (448, [(352, "D", ""), (224, "D", "G"), (256, "S", "")], 704, "F")
ROUND_FREE = (384, [(192, "S", "G"), (352, "S", "G"), (352, "S", "G")], 0, "")
FIN = [(0, 512), (512, 1024), (1024, H)]

SCRATCH = {
    "xs": ("sbuf", [128, 3 * Z], "bfloat16"),
    "xt": ("sbuf", [128, 4 * Z], "bfloat16"),
    "gq": ("sbuf", [128, 3 * Z], "bfloat16"),
    "pis": ("sbuf", [128, 4 * W], "int32"),
    "pio": ("sbuf", [128, 4 * W], "float16"),
    "pih": ("sbuf", [128, 3 * W], "float16"),
    "losti": ("sbuf", [128, 8], "int32"),
    "zeroi": ("sbuf", [128, W], "int32"),
    "zb": ("sbuf", [128, W], "bfloat16"),
    "zf": ("sbuf", [128, 2 * W], "float32"),
    "ci": ("sbuf", [128, 16], "int32"),
    "vz": ("sbuf", [128, 128], "bfloat16"),
    "cf": ("sbuf", [128, 64], "float32"),
    "mk": ("sbuf", [128, 80], "float32"),
    "row": ("sbuf", [128, 176], "float32"),
    "eb": ("sbuf", [128, 256], "bfloat16"),
    "en": ("sbuf", [128, 128], "bfloat16"),
    "ex": ("sbuf", [128, 128], "bfloat16"),
    "ef": ("sbuf", [128, 128], "float32"),
    "sa": ("sbuf", [128, 3 * 256], "float16"),
    "sb": ("sbuf", [128, 3 * 128], "float16"),
    "wq": ("sbuf", [128, 128], "bfloat16"),
    "wp": ("sbuf", [128, 4 * 256], "bfloat16"),
    "bx": ("sbuf", [128, 144], "bfloat16"),
    "bc": ("sbuf", [128, 144], "bfloat16"),
    "by": ("sbuf", [128, 144], "bfloat16"),
    "iw": ("sbuf", [128, ZS], "bfloat16"),
    "iz": ("sbuf", [128, Z], "bfloat16"),
    "inv": ("sbuf", [128, Z], "bfloat16"),
    "tab": ("sbuf", [128, 3 * ZS], "bfloat16"),
    "lst": ("sbuf", [128, 14 * W], "uint16"),
    "qn": ("sbuf", [128, ZS], "float32"),
    "va": ("sbuf", [128, ZS], "float32"),
    "vb": ("sbuf", [128, ZS], "float32"),
    "vd": ("sbuf", [128, Z], "float32"),
    "pn": ("sbuf", [128, Z], "float32"),
    "xf": ("sbuf", [128, H], "float32"),
    "xu": ("sbuf", [128, H], "float32"),
    "rb": ("sbuf", [128, H], "bfloat16"),
    "xj": ("sbuf", [128, H], "int32"),
    "xm": ("sbuf", [128, H], "int32"),
    "osend": ("sbuf", [128, H], "bfloat16"),
    "okeep": ("sbuf", [128, H], "bfloat16"),
    "oland": ("sbuf", [128, H], "bfloat16"),
    "ps": ("psum", [128, 4096], "float32"),
}
SEMAPHORES = (["eV", "eS", "eP", "eG", "sent", "api", "lpi", "llo", "lze", "go", "hop0", "hop1"] + ["lx%d" % i for i in range(4)]
              + ["at%d" % i for i in range(4)] + ["af%d" % i for i in range(4)] + ["st%d" % i for i in range(8)] + ["du%d" % i for i in range(70)])

LA, LB, LI, L0, LQ, LZ = 0, W, 2 * W, 3 * W, 10 * W, 13 * W
EX = 2048
PC = 2560
PD = 1024
TAB = {"pib": 0, "ta": ZS, "tb": 2 * ZS}


def send_order(q, T, topo):
    me = T.cores[q]
    others = [d for d in range(len(T.cores)) if d != q]
    off = [d for d in others if topo.chip(T.cores[d]) != topo.chip(me)]
    on = [d for d in others if d not in off]
    off.sort(key=lambda d: topo.die(T.cores[d]) != topo.die(me))
    return off, on


def helpers(q, T, topo):
    me = T.cores[q]
    off, _ = send_order(q, T, topo)
    h = [c for c in topo.cores_of(me) if c not in T.cores and topo.die(c) == topo.die(me)
         and all(topo.may_write(c, T.cores[d]) for d in off)]
    return h[:NHELP]


def tile_order(q, T, topo):
    off, on = send_order(q, T, topo)
    names = {"a": off[0], "b": off[1], "n": on[0], "o": q}
    return [names[c] for c in ORDER[q % 2]]


def expected(r, q, T, topo):
    off, on = send_order(r, T, topo)
    names = {"a": off[0], "b": off[1], "n": on[0], "o": r}
    return [names[c] for c in ARR[q]].index(q)


def bits(engines):
    m = 0
    for e in engines:
        m |= 1 << e
    return m


def pow2(lst):
    n = 1
    while 2 * n <= len(lst):
        n *= 2
    return lst[:n]


def small_engines(q, T, topo):
    me = T.cores[q]
    off, on = send_order(q, T, topo)
    used, small = [], {}
    for i, d in enumerate(off):
        e = topo.engines(me, T.cores[d])
        used += e
        n = len(e) // len(off)
        small[d] = pow2(e[i * n:(i + 1) * n])
    for i, d in enumerate(on):
        e = [k for k in topo.engines(me, T.cores[d]) if k not in used]
        n = len(small[off[0]])
        small[d] = e[i * n:(i + 1) * n]
    return small


def near_engines(q, T, topo):
    return topo.engines(T.cores[q], T.cores[send_order(q, T, topo)[1][0]])


def hop_engines(q, k, i, T, topo):
    e = near_engines(q, T, topo)
    if CUT[k][-1] < Z:
        far = topo.engines(T.cores[q], T.cores[send_order(q, T, topo)[0][k]])
        return pow2([x for x in e if x not in far])
    return e


def helper_program(g, core, T, topo):
    for q in range(len(T.cores)):
        hs = helpers(q, T, topo)
        if core in hs:
            i = hs.index(core)
            n = 0
            for k, d in enumerate(send_order(q, T, topo)[0]):
                c0, c1 = CUT[k][i], CUT[k][i + 1]
                g.wait_ge(T.sem["hop%d" % k], len(hop_engines(q, k, i, T, topo)))
                rid, pid, _ = topo.addr(T.cores[d])
                g.remote_dma(T.xt[:, q * Z + c0:q * Z + c1], T.xs[:, k * Z + c0:k * Z + c1], T.sem["at%d" % q], T.sem.sent,
                             pid, rid, topo.mask(core, T.cores[d]))
                n += len(topo.engines(core, T.cores[d]))
            if n:
                g.wait_ge(T.sem.sent, n)


def rank_program(g, core, T, topo):
    q = T.rank_of(core)
    if q is None:
        helper_program(g, core, T, topo)
        return
    N = len(T.cores)
    z, s = q // 2, q % 2
    A = AluOpType
    F = ActivationFunctionType
    eng = {"V": g.vector, "S": g.scalar, "P": g.tensor, "G": g, "Y": g.sync}
    cnt = {}
    waited = {e: {} for e in eng}
    log = {}

    def R(name, c0, c1, p0=0, p1=128, step=1):
        if name in TAB:
            return ("tab", p0, p1, TAB[name] + c0, TAB[name] + c1, step)
        return (name, p0, p1, c0, c1, step)

    def ap(r, pstep=1):
        if pstep > 1:
            return T[r[0]][r[1]:r[2]:pstep, r[3]:r[4]]
        if r[5] == 1:
            return T[r[0]][r[1]:r[2], r[3]:r[4]]
        return T[r[0]][r[1]:r[2], r[3]:r[4]:r[5]]

    def span(r):
        if r[0] == "ps":
            return (0, 128, r[3] // 512 * 512, (r[4] + 511) // 512 * 512)
        return r[1:5]

    def wait(e, tok):
        if waited[e].get(tok[0], 0) < tok[1]:
            eng[e].wait_ge(T.sem[tok[0]], tok[1])
            waited[e][tok[0]] = tok[1]

    def before(e, reads, writes):
        need = {}
        for rs, wr in ((reads, False), (writes, True)):
            for r in rs:
                a = span(r)
                for (b, bw, tok, be) in log.get(r[0], []):
                    if a[0] < b[1] and b[0] < a[1] and a[2] < b[3] and b[2] < a[3]:
                        if be == "P" and e == "P":
                            continue
                        if wr or bw or (r[0] == "ps" and be != e):
                            need[tok[0]] = max(need.get(tok[0], 0), tok[1])
        for k in need:
            wait(e, (k, need[k]))

    def after(e, reads, writes, tok):
        for rs, wr in ((reads, False), (writes, True)):
            for r in rs:
                log.setdefault(r[0], []).append((span(r), wr, tok, e))

    def op(e, fn, reads, writes):
        before(e, reads, writes)
        k = "e" + e
        cnt[k] = cnt.get(k, 0) + 1
        fn().then_inc(T.sem[k], 1)
        after(e, reads, writes, (k, cnt[k]))

    def dmas(e, sem, items):
        tok = (sem, cnt.get(sem, 0) + 16 * len(items))
        cnt[sem] = tok[1]
        for (o, i, rs, ws) in items:
            before(e, rs, ws)
            eng[e].dma_start(o, i).then_inc(T.sem[sem], 16)
        for (o, i, rs, ws) in items:
            after("D", rs, ws, tok)

    def landing(sem, n, regions):
        cnt[sem] = n
        after("D", [], regions, (sem, n))

    def sc(x):
        return ap(x) if isinstance(x, tuple) else x

    def regs(*xs):
        return [x for x in xs if isinstance(x, tuple)]

    def ts(out, in0, s1, op0, s2=None, op1=None):
        if op1 is None:
            op("V", lambda: g.vector.tensor_scalar(ap(out), ap(in0), sc(s1), None, op0), regs(in0, s1), [out])
        else:
            op("V", lambda: g.vector.tensor_scalar(ap(out), ap(in0), sc(s1), sc(s2), op0, op1), regs(in0, s1, s2), [out])

    def tt(out, in0, in1, o):
        op("V", lambda: g.vector.tensor_tensor(ap(out), ap(in0), ap(in1), o), [in0, in1], [out])

    def cp(e, out, in_):
        if e == "V":
            op("V", lambda: g.vector.tensor_copy(ap(out), ap(in_)), [in_], [out])
        else:
            op("S", lambda: g.scalar.activation(ap(out), ap(in_), F.Copy), [in_], [out])

    def act(out, in_, func=F.Identity, bias=0.0, scale=1.0):
        op("S", lambda: g.scalar.activation(ap(out), ap(in_), func, bias=sc(bias), scale=sc(scale)), regs(in_, bias, scale), [out])

    def plus(e, out, in_, v):
        if e == "V":
            ts(out, in_, v, A.add)
        else:
            act(out, in_, bias=v)

    def minus(e, out, in_):
        if e == "V":
            ts(out, in_, -1.0, A.mult)
        else:
            act(out, in_, scale=-1.0)

    def fill(out, v):
        op("V", lambda: g.vector.memset(ap(out), v), [], [out])

    def gather(e, out, win, lc, in1=None):
        off = R("lst", lc, lc + (out[4] - out[3]) // 16)
        if in1 is not None:
            op("V", lambda: g.vector.tensor_tensor(ap(out), ap(win).indirect(ap(off)), ap(in1), A.add), [win, off, in1], [out])
        elif e == "V":
            op("V", lambda: g.vector.tensor_copy(ap(out), ap(win).indirect(ap(off))), [win, off], [out])
        else:
            op("S", lambda: g.scalar.activation(ap(out), ap(win).indirect(ap(off)), F.Copy), [win, off], [out])

    def mms(items):
        reads = [i[1] for i in items] + [i[2] for i in items]
        writes = [i[0] for i in items]

        def fn():
            ins = None
            for (o, l, r, a, b) in items:
                ins = g.tensor.matmul(ap(o), ap(l), ap(r), a, b)
            return ins
        op("P", fn, reads, writes)

    def col(i, n=1):
        return R("cf", i, i + n)

    ndma = [0]

    def copies(pairs, pstep=1):
        dmas("Y", "du%d" % ndma[0], [(ap(o, pstep), ap(i, pstep), [i], [o]) for (o, i) in pairs])
        ndma[0] += 1

    def crossed(buf, c0, c1):
        return [(R(buf, H + c0, H + c1, 64 * (1 - h), 64 * (2 - h)), R(buf, c0, c1, 64 * h, 64 * h + 64)) for h in range(2)]

    off, on = send_order(q, T, topo)
    order = off + on
    small_e = small_engines(q, T, topo)
    slot = {d: i for i, d in enumerate(order)}
    data = N - 1

    landing("api", sum(len(small_engines(r, T, topo)[q]) for r in range(data) if r != q),
            [R("pih", r * W, (r + 1) * W) for r in range(data) if r != q])
    for r in range(N):
        if r != q:
            if r in on:
                n = len(near_engines(r, T, topo))
            else:
                own = [T.cores[r]] if CUT[send_order(r, T, topo)[0].index(q)][-1] < Z else []
                n = sum(len(topo.engines(c, core)) for c in helpers(r, T, topo) + own)
            landing("at%d" % r, n, [R("xt", r * Z, (r + 1) * Z)])
    mate = q ^ 1
    fin_e = topo.engines(core, T.cores[mate])
    for i, (c0, c1) in enumerate(FIN):
        landing("af%d" % i, len(topo.engines(T.cores[mate], core)), [R("oland", c0, c1)])

    def pi_of(r, c0, c1):
        if r == q:
            b = 2 * s + z
            return R("pio", b * W + c0, b * W + c1)
        return R("pih", r * W + c0, r * W + c1)

    if q < data:
        its = [(T.pis[64 * t:64 * t + 64, 2 * W * u:2 * W * (u + 1)], T.pi[64 * u:64 * u + 64, 2 * W * t:2 * W * (t + 1)],
                [], [R("pis", 2 * W * u, 2 * W * (u + 1), 64 * t, 64 * t + 64)]) for t in range(2) for u in range(2)]
        dmas("Y", "lpi", its[:2])
        dmas("S", "lpi", its[2:])
        after("D", [], [R("pis", 0, 4 * W)], ("lpi", cnt["lpi"]))
    dmas("S", "llo", [(T.losti[64 * t:64 * t + 64, 0:2], T.lost[64 * s:64 * s + 64, :], [], [R("losti", 0, 2, 64 * t, 64 * t + 64)]) for t in range(2)])
    dmas("Y", "lze", [(T.zeroi[64 * t:64 * t + 64, :], T.zero[64 * s:64 * s + 64, :], [], [R("zeroi", 0, W, 64 * t, 64 * t + 64)]) for t in range(1 + s)])
    seq = tile_order(q, T, topo)
    sent = [0]

    def load(d):
        buf, c = ("xt", q * Z) if d == q else ("xs", slot[d] * Z)
        dz, ds = d // 2, d % 2
        dmas("Y", "lx%d" % d, [(T[buf][64 * t:64 * t + 64, c:c + Z], T.x[64 * ds:64 * ds + 64, (2 * t + dz) * Z:(2 * t + dz + 1) * Z],
                                [], [R(buf, c, c + Z, 64 * t, 64 * t + 64)]) for t in range(2)])

    def send(c):
        k = "ab".find(c.lower())
        d = off[k] if k >= 0 else on[0]
        at = slot[d] * Z
        before("G", [R("xs", at, at + Z)], [])
        if c.islower():
            c0 = CUT[k][-1] if k >= 0 else 0
            e = topo.engines(core, T.cores[d])
            rid, pid, _ = topo.addr(T.cores[d])
            g.remote_dma(T.xt[:, q * Z + c0:(q + 1) * Z], T.xs[:, at + c0:at + Z], T.sem["at%d" % q], T.sem.sent, pid, rid, bits(e))
            sent[0] += len(e)
            return
        trs = []
        for i, hc in enumerate(helpers(q, T, topo)):
            rid, pid, _ = topo.addr(hc)
            c0, c1 = CUT[k][i], CUT[k][i + 1]
            e = hop_engines(q, k, i, T, topo)
            trs.append(RemoteDMATransfer(dst_ids=[DstId(rid=rid, pnc=pid)], dma_engine_mask=bits(e), remote_sem=T.sem["hop%d" % k],
                                         src=T.xs[:, at + c0:at + c1], dst=T.xs[:, k * Z + c0:k * Z + c1]))
            sent[0] += len(e)
        for t in trs:
            g.remote_dma_fused([t], local_sem=T.sem.sent)

    for d in seq[:FIRST]:
        load(d)
    op("G", lambda: g.iota(T.ci[:, 0:2], [[64, 2]], 0, 1), [], [R("ci", 0, 2)])
    op("G", lambda: g.iota(T.row[:], [[1, 176]], -16, 0, allow_small_or_imprecise_dtypes=True), [], [R("row", 0, 176)])
    op("G", lambda: g.iota(T.inv[:, 0:GZ], [[0, GZ]], 0, 0, allow_small_or_imprecise_dtypes=True), [], [R("inv", 0, GZ)])

    EQ = 32
    fill(R("eb", 0, 256), 0.0)
    p, p2 = R("ci", 0, 1), R("ci", 0, 2)
    ts(R("ci", 2, 3), p, 15, A.bitwise_and)
    ts(R("ci", 3, 4), p, 6, A.arith_shift_right)
    ts(R("ci", 4, 5), p, 63, A.bitwise_and)
    cp("V", col(4, 2), R("ci", 2, 4))
    ts(R("ci", 5, 6), p, 48, A.bitwise_and)
    ts(col(EQ, 16), R("row", 16, 32), col(4), A.is_equal)
    ts(R("ci", 6, 8), p2, 112, A.bitwise_and)
    ts(col(6), col(EQ), col(EQ + 1), A.add, col(EQ + 4), A.add)
    ts(col(8), col(EQ + 1), col(5), A.mult, col(EQ + 4), A.add)
    ts(R("mk", 0, 65), R("row", 16, 81), col(6), A.mult)
    ts(col(9), col(8), 20.0, A.mult)
    ts(R("ci", 8, 10), p2, 127, A.bitwise_and)
    ts(R("ci", 10, 12), p2, 4, A.arith_shift_right, 4, A.bitwise_and)
    ts(col(15, 3), R("row", 16, 22, step=2), col(5), A.add)
    cp("V", col(56, 8), R("ci", 4, 12))
    ts(col(10), col(EQ), col(EQ + 4), A.subtract, 20.0, A.mult)
    ts(col(49), col(EQ + 1), 64.0, A.mult, col(EQ + 8), A.add)
    if q < data:
        mine = (2 * s + z) * W
        parts = [(c0, c1) for (c0, c1) in ((0, mine), (mine + W, 4 * W)) if c0 < c1]
        for (c0, c1) in parts + [(mine, mine + W)]:
            ts(R("pio", c0, c1), R("pis", c0, c1), -1280.0, A.add)
        before("G", [R("pio", c0, c1) for (c0, c1) in parts], [])
        trs = []
        for d in order:
            rid, pid, _ = topo.addr(T.cores[d])
            b = 2 * (d % 2) + d // 2
            trs.append(RemoteDMATransfer(dst_ids=[DstId(rid=rid, pnc=pid)], dma_engine_mask=bits(small_e[d]), remote_sem=T.sem.api,
                                         src=T.pio[:, b * W:(b + 1) * W], dst=T.pih[:, q * W:(q + 1) * W]))
            sent[0] += len(small_e[d])
        g.remote_dma_fused(trs, local_sem=T.sem.sent)
    for c in SENDS[s][:EARLY]:
        send(c)
    if FIRST < N:
        g.sem_inc(T.sem.go, 1)
        g.sync.wait_ge(T.sem.go, 1)
    for d in seq[FIRST:]:
        load(d)
    for c in SENDS[s][EARLY:]:
        send(c)

    for buf in ("qn", "va", "vb"):
        op("G", lambda buf=buf: g.iota(T[buf][:, Z:Z + 1], [[0, 1]], 0, 0, allow_small_or_imprecise_dtypes=True), [], [R(buf, Z, Z + 1)])
    op("G", lambda: g.iota(T.vz[:], [[0, 128]], 0, 0, allow_small_or_imprecise_dtypes=True), [], [R("vz", 0, 128)])
    act(R("iw", 0, 64), R("row", 16, 80), bias=col(9), scale=col(EQ + 8))
    act(col(12), col(5), bias=1.0, scale=-1.0)
    if s == 1:
        act(R("zf", 0, W), R("row", 16, 16 + W), bias=col(4), scale=16.0)
    for k in range(1, 4):
        act(R("iw", 64 * k, 64 * k + 64), R("iw", 0, 64), bias=R("mk", k, k + 1))
    for k in range(1, 5):
        act(R("iw", 256 * k, 256 * k + 256), R("iw", 0, 256), bias=R("mk", 4 * k, 4 * k + 1))

    def q_list(r):
        ts(R("lst", LQ + r * W, LQ + (r + 1) * W), pi_of(r, 0, W), 1280.0, A.add)

    def tile_part(e, r, c0, c1):
        gather(e, R("gq", r * Z + c0, r * Z + c1), R("xt", r * Z, (r + 1) * Z), LQ + r * W + c0 // 16)
    ZV = ZVS[q == data]
    early = int(s == 0 and q in seq[:FIRST])
    act(R("iw", H, Z), R("iw", 0, H), bias=col(10))
    if s == 1:
        ts(R("zf", W, 2 * W), R("zeroi", 0, W), float(Z), A.mult)
        cp("V", R("iw", Z, Z + 1), R("mk", 64, 65))
    else:
        q_list(q)
    cp("V", col(13, 2), R("losti", 0, 2))
    if s == 1:
        tt(R("zf", 0, W), R("zf", 0, W), R("zf", W, 2 * W), A.max)
    ts(R("eb", 64, 128), R("row", 16, 80), col(56), A.is_equal)
    ts(R("eb", 128, 192), R("row", 16, 80), col(56), A.is_equal)
    if s == 1:
        cp("V", R("lst", LZ, LZ + W), R("zf", 0, W))
        gather("S", R("iz", ZV, Z), R("iw", 0, Z + 1), LZ + ZV // 16)
    elif early:
        tile_part("S", q, OWN, Z)
    ts(col(18, 3), col(15, 3), col(13 + s), A.is_equal)
    ts(col(21, 3), col(15, 3), col(14 - s), A.is_equal)
    if s == 0:
        ts(R("zb", 0, W, 0, 64), R("zeroi", 0, W, 0, 64), 4096.0, A.mult)
    for r in range(data):
        ts(R("sa", 256 * r, 256 * r + 256), R("eb", 0, 256), col(18 + r), A.mult)
    tt(col(24, 3), col(18, 3), col(21, 3), A.add)
    for r in range(data):
        ts(R("sb", 128 * r, 128 * r + 128), R("eb", 64, 192), col(21 + r), A.mult)
    ts(col(27, 3), col(24, 3), -1.0, A.add)
    if s == 1 and q < data:
        q_list(q)
    fill(R("inv", GZ, Z), 0.0)
    for r in range(N):
        ts(R("wp", 256 * r, 256 * r + 256), R("eb", 0, 256), col(27 + r if r < data else 12), A.mult)
    ts(R("wq", 0, 128), R("eb", 64, 192), col(5), A.mult)
    ts(R("by", 0, 80), R("row", 0, 80), col(57), A.is_equal, col(49), A.mult)
    ts(R("by", 80, 144), R("row", 16, 80), col(57), A.is_equal, col(49), A.mult)
    if early:
        tile_part("V", q, 0, OWN)
    if s == 1:
        gather("V", R("iz", 0, ZV), R("iw", 0, Z + 1), LZ)

    arrive = sorted(range(N), key=lambda r: expected(r, q, T, topo))
    gl = [r for r in arrive if r < data]

    mms([(R("ps", EX, EX + 80), R("sa", 256 * r + 128 * (1 - h), 256 * r + 128 * (2 - h)), pi_of(r, 80 * h, 80 * h + 80),
          r == 0 and h == 0, r == data - 1 and h == 1) for r in range(data) for h in range(2)])
    mms([(R("ps", 0, W), R("sb", 128 * r, 128 * r + 128), pi_of(r, 0, W), r == 0, r == data - 1) for r in range(data)])
    ts(R("lst", LA, LA + 80), R("ps", EX, EX + 80), 1280.0, A.add)
    ts(R("lst", LB, LB + W), R("ps", 0, W), 1280.0, A.add)
    if gl[0] != q:
        q_list(gl[0])
    op("V", lambda: g.vector.tensor_copy(T.inv[:, 0:Z].indirect(T.lst[:, LA:LA + 80]), T.iw[:, 0:H]),
       [R("iw", 0, H), R("lst", LA, LA + 80)], [R("inv", 0, Z)])
    gather("S", R("pib", 0, Z), R("iz" if s else "iw", 0, Z), LB)

    grp = {}

    def flags(key, total):
        grp[key] = grp.get(key, 0) + 1
        return grp[key] == 1, grp[key] == total

    def q_mm(r, banks=range(5)):
        src, wt = ("gq", R("wp", 256 * r + 64, 256 * r + 192)) if r < data else ("xt", R("wq", 0, 128))
        mms([(R("ps", 512 * b, 512 * b + 512), wt, R(src, r * Z + 512 * b, r * Z + 512 * b + 512)) + flags(("q", b), N) for b in banks])

    emitted = []

    def p_mm(r, chunks):
        for (c0, c1) in chunks:
            if (r, c0) not in emitted:
                emitted.append((r, c0))
                mms([(R("ps", PC + c0, PC + c1), R("wp", 256 * r + 128 * (1 - h), 256 * r + 128 * (2 - h)),
                      R("xt", r * Z + H * h + c0, r * Z + H * h + c1)) + flags(("p", c0), 2 * N) for h in range(2)])

    def sums(r, banks):
        if len(banks) > 3:
            p_mm(r, FIN)
        if r == data:
            todo = [b for b in banks if (r, -1 - b) not in emitted]
            emitted.extend((r, -1 - b) for b in todo)
            for i in range(0, len(todo), 2):
                q_mm(r, todo[i:i + 2])

    plan = [ROUND_PTR] * (5 - NPRE[s]) + [ROUND_END] + [ROUND_FREE] * (1 + NPRE[s]) + [(0, [], 0, "")]

    def extract(tab, c0, c1, at, mat="bx"):
        mms([(R("ps", at, at + (c1 - c0) // 16), R(mat, 16 - r, 144 - r), R(tab, c0 + r, c1, step=16), r == 0, r == 15) for r in range(16)])

    pend, late, cross = [], [], []

    def flush():
        while pend:
            lc, n, at = pend.pop(0)
            ts(R("lst", lc, lc + n), R("ps", at, at + n), float(Z), A.min)

    tabs = ["ta", "tb"]
    level = [-1]
    fresh = ["ta", "tb"]

    def double(at, nv):
        n = level[0]
        src, lin = (tabs[n % 2], L0 + W * n) if n >= 0 else ("pib", LI)
        dst, lout = tabs[(n + 1) % 2], L0 + W * (n + 1)
        level[0] += 1
        win = R(src, 0, Z + 1)
        gather("S", R(dst, nv, H), win, lin + nv // 16)
        gather("V", R(dst, 0, nv), win, lin)
        copies(crossed(dst, 0, H), 1 if dst in fresh else 4)
        if dst in fresh:
            fresh.remove(dst)
        extract(dst, 0, H, at)
        pend.append((lout, 80, at))
        cross.append((dst, lout, plan[n + 2][0]))

    gs = gl[early:]
    if early:
        q_mm(q, range(4))
    for r in arrive[:PRE[q]]:
        sums(r, range(4))
    mms([(R("ps", EX, EX + W), R("by", 16 - r, 144 - r), R("inv", r, Z, step=16), r == 0, r == 15 and s == 1) for r in range(16)])
    if s == 0:
        mms([(R("ps", EX, EX + W), R("eb", 64, 192, 0, 64), R("zb", 0, W, 0, 64), False, True)])
    for r in gl[1:]:
        if r != q:
            q_list(r)
    tile_part("S", gs[0], T0, Z)
    ts(col(28 + 22, 2), col(62, 2), col(4), A.is_equal, 64.0, A.mult)
    ts(R("tab", Z, 3 * ZS, step=ZS), R("row", 0, 3), 0.0, A.mult, R("mk", 64, 65), A.add)
    ts(col(30, 2), col(50, 2), col(EQ + 8), A.add)
    ts(R("ex", 0, 128), R("row", 16, 144), col(61), A.is_equal)
    ts(R("bx", 0, 144), R("row", 0, 144), col(58), A.is_equal, col(30), A.mult)
    ts(R("bc", 0, 144), R("row", 0, 144), col(59), A.is_equal, col(31), A.mult)
    ts(R("ef", 0, 128), R("row", 16, 144), col(60), A.is_equal)
    for (c0, c1, at, h) in ((0, 80, 80, 1), (0, W, 0, 0), (80, W, 0, 1)):
        ts(R("lst", LI + c0, LI + c1, 64 * h, 64 * h + 64), R("ps", EX + at, EX + at + c1 - c0, 64 * h, 64 * h + 64), float(Z), A.min)
    sums(arrive[PRE[q]], range(4))
    q_mm(gs[0], (2, 3))
    double(EX + 256, 608)
    sums(arrive[PRE[q] + 1], range(4))
    tile_part("V", gs[0], 0, T0)
    if not early:
        tile_part("S", gs[1], 1536, Z)
    flush()
    q_mm(gs[0], (0, 1))
    if not early:
        tile_part("S", gs[1], T1, 1536)
        tile_part("V", gs[1], 0, T1)
    for k in range(NPRE[s]):
        double(EX + 256, 608)
    tile_part("S", gl[2], 1536, Z)
    tile_part("V", gl[2], 0, 512)
    flush()
    tile_part("V", gl[2], 512, 1024)
    tile_part("V", gl[2], 1024, 1536)
    if early:
        q_mm(q, (4,))
    q_mm(gs[0], (4,))
    if not early:
        q_mm(gs[1], (3, 4))
    for r in arrive[:-1]:
        sums(r, range(5))
    if not early:
        q_mm(gs[1], (0, 1, 2))
    p_mm(arrive[-1], FIN[:2])
    plus("S", R("pn", 0, 1024), R("ps", PC, PC + 1024), LIFT)
    q_mm(gl[2], (0,))
    sums(data, (0, 3, 4))
    q_mm(gl[2], (3, 4))
    sums(data, (1, 2))
    q_mm(gl[2], (1,))
    q_mm(gl[2], (2,))
    p_mm(arrive[-1], FIN)
    minus("V", R("qn", 0, 512), R("ps", 0, 512))
    minus("S", R("qn", 1536, Z), R("ps", 1536, Z))
    minus("V", R("qn", 512, 1024), R("ps", 512, 1024))
    minus("V", R("qn", 1024, 1536), R("ps", 1024, 1536))
    plus("S", R("pn", 1024, H), R("ps", PC + 1024, PC + H), LIFT)
    copies(crossed("pn", H - plan[0][0], H))
    for i, (dst, lout, C) in enumerate(cross):
        if i + 1 < len(cross):
            extract(dst, H - C, H, 2048 + 64 * i, "bc")
            pend.append((lout + (Z - C) // 16, C // 16, 2048 + 64 * i))
        else:
            extract(dst, H - C, H, 128 - C // 16, "bc")
            late.append(C // 16)

    def dup(e, buf, c0, c1):
        if e == "G":
            op("G", lambda: g.affine_select(T.vd[:, c0:c1], T[buf][:, c0:c1], [[0, c1 - c0]], A.is_ge, 0.0, 0, 0), [R(buf, c0, c1)], [R("vd", c0, c1)])
        else:
            copies([(R("vd", c0, c1), R(buf, c0, c1))])

    def one_round(win, add, dst, lc, now, nxt):
        C, cuts, B, when = now
        n = level[0]
        src, tb, lin, lout = tabs[n % 2], tabs[(n + 1) % 2], L0 + W * n, L0 + W * (n + 1)
        w = R(win, 0, Z + 1)

        def part(c0, c1):
            gather("V", R(dst, c0, c1), w, lc + c0 // 16, R(add, c0, c1))

        def jump(c0, c1):
            gather("S", R(tb, c0, c1), R(src, 0, Z + 1), lin + c0 // 16)

        def over(c0, c1):
            if n < 5:
                copies(crossed(tb, c0, c1), 1 if tb in fresh else 4)

        def second():
            extract(tb, B, H, 512)
            pend.append((lout + B // 16, (H - B) // 16, 512))
            if n < 5:
                Cn = plan[n + 2][0]
                extract(tb, H - Cn, H, 128 - Cn // 16, "bc")
                late.append(Cn // 16)
        if when:
            level[0] += 1
        if "F" in when:
            jump(0, B)
        c = done = 0
        for i, (k, who, twin) in enumerate(cuts):
            part(c, c + k)
            if who == "D":
                copies(crossed(dst, c, c + k))
            else:
                for (o, x) in crossed(dst, c, c + k):
                    cp("S", o, x)
            c += k
            if twin:
                dup(twin, dst, done, c)
                done = c
            if i == 1:
                flush()
                if "F" in when:
                    jump(B, H)
            if i == 1 and "F" in when:
                over(0, B)
                extract(tb, 0, B, 128)
        if when:
            k = late.pop() if late else 0
            pend.append((lout - k, k + B // 16, 128 - k))
        part(H - C, H)
        dup("G", dst, done, H)
        part(Z - C, Z)
        if nxt[0]:
            dup("Y", dst, Z - nxt[0], Z)
        flush()
        if "P" in when:
            cs = [(B, H)] if H - B <= 512 else [(B, B + 512), (B + 512, H)]
            mms([(R("ps", 1024 + c0 - B, 1024 + c1 - B), R("ex", 0, 128), R(tb, c0, c1), True, True) for (c0, c1) in cs])
            cp("S", R(tb, H + B, Z), R("ps", 1024, 1024 + H - B))
        if "F" in when:
            second()
        if when and tb in fresh:
            fresh.remove(tb)

    vs = ["va", "vb"]
    op("G", lambda: g.affine_select(T.en[:], T.vz[:, 0:128], [[-1, 128]], A.not_equal, -1.0, 0, 1), [R("vz", 0, 128)], [R("en", 0, 128)])
    one_round("qn", "pn", "va", LI, plan[0], plan[1])
    again = [(at, c0, c1) for at in (PC, PD) for (c0, c1) in FIN]
    for b in range(6):
        one_round(vs[b % 2], "vd", vs[(b + 1) % 2], L0 + W * b, plan[b + 1], plan[b + 2])
        while again and (b == 4 or len(again) > max(3, 5 - b)):
            at, c0, c1 = again.pop(0)
            mms([(R("ps", at + c0, at + c1), R("ef", 0, 128), R("pn", c0, c1), True, False)])
    flush()

    rid, pid, _ = topo.addr(T.cores[mate])

    def last(out, i):
        c0, c1 = FIN[i]
        gather("V", R(out, c0, c1), R(vs[0], 0, Z + 1), L0 + 6 * W + c0 // 16, R("vd", c0, c1))

    def floor256(i):
        c0, c1 = FIN[i]
        act(R("xu", c0, c1), R("xf", c0, c1), bias=TOP - 128.0, scale=1.0 + 2.0 ** -20)
        act(R("ps", c0, c1), R("xu", c0, c1), bias=-TOP)

    def hand(i):
        c0, c1 = FIN[i]
        before("G", [R("osend", c0, c1)], [])
        g.remote_dma(T.oland[:, c0:c1], T.osend[:, c0:c1], T.sem["af%d" % i], T.sem.sent, pid, rid, bits(fin_e))
        sent[0] += len(fin_e)
        mms([(R("ps", PC + c0, PC + c1), R("en", 0, 128), R("osend", c0, c1), False, True)])
        mms([(R("ps", PD + c0, PD + c1), R("en", 0, 128), R("osend", c0, c1), False, False)])

    def rest(i):
        c0, c1 = FIN[i]
        tt(R("osend", c0, c1), R("xf", c0, c1), R("ps", c0, c1), A.subtract)
        hand(i)

    def by_bits(i):
        c0, c1 = FIN[i]
        ts(R("xm", c0, c1), R("xj", c0, c1), 255, A.bitwise_and)
        cp("V", R("osend", c0, c1), R("xm", c0, c1))
        hand(i)

    def keep_round(e, i):
        c0, c1 = FIN[i]
        plus(e, R("rb", c0, c1), R("ps", PC + c0, PC + c1), 49152.0 - 127.5)
        mms([(R("ps", PD + c0, PD + c1), R("en", 0, 128), R("rb", c0, c1), False, True)])

    def store(e, sem, buf, rows, i):
        c0, c1 = FIN[i]
        dmas(e, sem, [(T.y[64 * rows:64 * rows + 64, H * h + c0:H * h + c1], T[buf][64 * h:64 * h + 64, c0:c1],
                       [R(buf, c0, c1, 64 * h, 64 * h + 64)], []) for h in range(2)])

    def keep(e, i):
        c0, c1 = FIN[i]
        plus(e, R("okeep", c0, c1), R("ps", PD + c0, PD + c1), 49152.0)
        store("S", "st%d" % i, "okeep", s, i)

    last("xf", 0)
    floor256(0)
    last("xf", 1)
    floor256(1)
    last("xj", 2)
    rest(0)
    by_bits(2)
    rest(1)
    keep_round("S", 0)
    keep_round("V", 2)
    keep_round("V", 1)
    keep("S", 0)
    keep("V", 2)
    keep("V", 1)
    for i in (0, 2, 1):
        store("Y", "st%d" % (4 + i), "oland", 1 - s, i)
    cnt["sent"] = sent[0]
    for k in cnt:
        if cnt[k]:
            wait("G", (k, cnt[k]))
